import numpy as np
import ml_dtypes


def mxq(x, axis, fmt="e4m3"):
    dtype, down = {"e4m3": (ml_dtypes.float8_e4m3fn, 7), "e5m2": (ml_dtypes.float8_e5m2, 14)}[fmt]
    v = np.moveaxis(np.asarray(x, np.float32).astype(ml_dtypes.bfloat16).astype(np.float64), axis, -1)
    blocks = v.reshape(v.shape[:-1] + (-1, 32))
    amax = np.abs(blocks).max(-1, keepdims=True)
    byte = np.maximum(np.where(amax > 0, np.frexp(amax)[1] - 1 + 127, 0) - down, 1)
    scale = np.exp2(byte - 127.0)
    codes = (blocks / scale).astype(np.float32).astype(dtype).astype(np.float64)
    return np.moveaxis((codes * scale).reshape(v.shape), -1, axis)


WIDE = False


def mx_kscale(k):
    if not WIDE:
        return np.ones(k)
    levels = np.array([24, -24, 12, -12, 0])
    if k % 512:
        return np.exp2(np.random.permutation(np.resize(levels, k // 32))).repeat(32)
    a = np.empty((k // 512, 16))
    for p in range(k // 512):
        a[p, :8] = np.random.permutation(np.resize(levels, 8))
        for g in range(8):
            far = levels[np.abs(levels - a[p, g]) >= 10]
            a[p, g + 8] = far[np.random.randint(len(far))]
    return np.exp2(a.ravel()).repeat(32)


def f64(x):
    return np.asarray(x).astype(np.float64)


def striped(idx):
    return np.tile(idx.reshape(-1, 16).T, (8, 1)).astype(np.uint16)


def unstriped(offs):
    return offs[:16].T.reshape(-1).astype(np.int64)


E2M1 = np.array([0.0, 0.5, 1.0, 1.5, 2.0, 3.0, 4.0, 6.0, -0.0, -0.5, -1.0, -1.5, -2.0, -3.0, -4.0, -6.0])


def pack_weight(w, fmt):
    k, n = w.shape
    w = f64(np.asarray(w, np.float32).astype(ml_dtypes.bfloat16)).reshape(k // 32, 32, n)
    amax = np.abs(w).max(1)
    if fmt == "e4m3":
        byte = np.frexp(amax)[1] - 1 + 127 - 7
    else:
        mant, ex = np.frexp(amax / 6.0)
        byte = np.where(mant > 0.5, ex, ex - 1) + 127
    byte = np.clip(np.where(amax > 0, byte, 1), 1, 254)
    scaled = (w * np.exp2(127.0 - byte)[:, None, :]).reshape(k, n).astype(np.float32)
    by_word = np.ascontiguousarray(scaled.reshape(k // 512, 128, 4, n).transpose(0, 1, 3, 2))
    if fmt == "e4m3":
        words = by_word.astype(ml_dtypes.float8_e4m3fn).view(np.uint8)
    else:
        c = by_word.astype(ml_dtypes.float4_e2m1fn).view(np.uint8) & 0xF
        words = (c[..., 0::2] | (c[..., 1::2] << 4)).reshape(k // 512, 128, 2 * n)
    return np.ascontiguousarray(words), np.ascontiguousarray(byte.astype(np.uint8).reshape(k // 512, 16, n))


def unpack_weight(words, scales, fmt):
    g, _, n = scales.shape
    words = np.ascontiguousarray(words).reshape(g, 128, n, -1)
    if fmt == "e4m3":
        vals = words.view(ml_dtypes.float8_e4m3fn).astype(np.float64)
    else:
        nib = np.empty((g, 128, n, 4), np.uint8)
        nib[..., 0::2] = words & 0xF
        nib[..., 1::2] = words >> 4
        vals = E2M1[nib]
    vals = vals * np.repeat(np.exp2(scales.astype(np.float64) - 127.0), 8, axis=1)[..., None]
    return vals.transpose(0, 1, 3, 2).reshape(g * 512, n)


K, R, N, T, J = 512, 512, 512, 2048, 512


def setup_inputs():
    n = np.random.standard_normal
    s = mx_kscale(K)[:, None]
    u = mx_kscale(R)[:, None]
    p_tab = pack_weight(n((K, T)) * s, "e4m3")
    p_w = pack_weight(n((K, R)) / np.sqrt(K) / s * u.T, "e2m1")
    p_wd = pack_weight(n((R, N)) / np.sqrt(R) / u, "e4m3")
    return {
        "tab_words": p_tab[0],
        "tab_scales": p_tab[1],
        "c": (n((K, J)) * s).astype(np.float32),
        "w_words": p_w[0],
        "w_scales": p_w[1],
        "wc": (n((K, R)) / np.sqrt(K) / s * u.T).astype(np.float32),
        "wd_words": p_wd[0],
        "wd_scales": p_wd[1],
        "res": (n((N, J))).astype(np.float32),
        "offs": striped(np.concatenate([np.random.permutation(T)[:J] for _ in range(3)])),
    }


def reference(tab_words, tab_scales, c, w_words, w_scales, wc, wd_words, wd_scales, res, offs):
    idx = unstriped(offs).reshape(3, J)
    tab_ = unpack_weight(tab_words, tab_scales, "e4m3")[:, idx]
    c_ = mxq(f64(c), 0, "e4m3")
    w_ = unpack_weight(w_words, w_scales, "e2m1")
    a0 = w_.T @ tab_[:, 0]
    a1 = w_.T @ tab_[:, 1]
    a2 = w_.T @ tab_[:, 2]
    wc_ = mxq(f64(wc), 0, "e4m3")
    ac = wc_.T @ c_
    h = np.maximum(np.maximum(np.maximum(a0, a1), a2) + ac, 0.0)
    h_ = mxq(h, 0, "e4m3")
    wd_ = unpack_weight(wd_words, wd_scales, "e4m3")
    y = wd_.T @ h_
    return f64(res) + y

@@ -1,0 +1,217 @@
+from contextlib import ExitStack
+
+import concourse.mybir as mybir
+from concourse.masks import make_identity
+
+K, R, N, T, J = 512, 512, 512, 2048, 512
+G = 3
+FLOPS = 2 * 512 * 512 * 512 * 5
+
+F32 = mybir.dt.float32
+BF16 = mybir.dt.bfloat16
+I32 = mybir.dt.int32
+U32 = mybir.dt.uint32
+U16 = mybir.dt.uint16
+U8 = mybir.dt.uint8
+FP8X4 = mybir.dt.float8_e4m3fn_x4
+FP4X4 = mybir.dt.float4_e2m1fn_x4
+ACT = mybir.ActivationFunctionType
+ALU = mybir.AluOpType
+
+P = 128
+PACK = 4
+CHUNK = 128
+HALF = 256
+
+
+def load_plane(nc, plane, rows):
+    for q in range(4):
+        nc.sync.dma_start(out=plane[32 * q : 32 * q + 4, :].bitcast(I32), in_=rows[4 * q : 4 * q + 4, :].bitcast(I32))
+
+
+def interleave(nc, grouped, raw):
+    nc.scalar.activation(
+        out=grouped.rearrange("p (c i) t -> p c t i", i=4),
+        in_=raw.rearrange("p t (c i) -> p c t i", i=4),
+        func=ACT.Copy,
+    )
+
+
+def tile_list_pnet_res_kernel(
+    tc, tab_words, tab_scales, c, w_words, w_scales, wc, wd_words, wd_scales, res, offs, out
+):
+    nc = tc.nc
+    with ExitStack() as ctx:
+        keep = ctx.enter_context(tc.tile_pool(name="keep", bufs=1))
+        work = ctx.enter_context(tc.tile_pool(name="work", bufs=4))
+        psum = ctx.enter_context(tc.psum_pool(name="psum", bufs=2))
+
+        offsets = keep.tile([P, G * J // 16], U16, name="offsets")
+        tab_plane = keep.tile([P, T], U8, name="tab_plane", align_bytes=64)
+        w_plane = keep.tile([P, R], U8, name="w_plane", align_bytes=64)
+        wd_plane = keep.tile([P, N], U8, name="wd_plane", align_bytes=64)
+        nc.vector.memset(tab_plane[:].bitcast(I32), 0)
+        nc.vector.memset(w_plane[:].bitcast(I32), 0)
+        nc.vector.memset(wd_plane[:].bitcast(I32), 0)
+        ident = keep.tile([P, P], F32, name="ident")
+        make_identity(nc, ident[:])
+
+        def load_half(name, rows, h):
+            raw = keep.tile([P, PACK, HALF], F32, name="raw", tag="%s%d" % (name, h))
+            nc.sync.dma_start(out=raw[:], in_=rows.rearrange("(p t) r -> p t r", t=PACK)[:, :, h * HALF : (h + 1) * HALF])
+            return raw
+
+        nc.sync.dma_start(offsets[:], offs)
+        wc_raw = [load_half("wc", wc, 0)]
+        load_plane(nc, tab_plane, tab_scales[0])
+        wc_raw.append(load_half("wc", wc, 1))
+        w_codes = keep.tile([P, 2 * R], U8, name="w_codes", align_bytes=64)
+        nc.sync.dma_start(out=w_codes[:].bitcast(I32), in_=w_words[0].bitcast(I32))
+        table = keep.tile([P, T], I32, name="table", align_bytes=64)
+        nc.sync.dma_start(out=table[:], in_=tab_words[0].rearrange("p t i -> p (t i)").bitcast(I32))
+        load_plane(nc, w_plane, w_scales[0])
+        c_raw = [load_half("c", c, h) for h in range(2)]
+        wd_codes = keep.tile([P, N], I32, name="wd_codes", align_bytes=64)
+        nc.sync.dma_start(out=wd_codes[:], in_=wd_words[0].rearrange("p n i -> p (n i)").bitcast(I32))
+        load_plane(nc, wd_plane, wd_scales[0])
+        res_sb = []
+        for h in range(2):
+            rows = keep.tile([P, N // P, HALF], F32, name="res%d" % h)
+            nc.sync.dma_start(out=rows[:], in_=res.rearrange("(b p) j -> p b j", p=P)[:, :, h * HALF : (h + 1) * HALF])
+            res_sb.append(rows)
+        out_rows = out.rearrange("(b p) j -> p b j", p=P)
+
+        picked_plane = keep.tile([P, G * J], U8, name="picked_plane", align_bytes=64)
+        nc.vector.tensor_copy(picked_plane[:], tab_plane[:].indirect(offsets[:]))
+
+        def quantize(name, bf, width):
+            codes = keep.tile([P, width], U32, name=name + "_codes", align_bytes=64)
+            plane = keep.tile([P, width], U8, name=name + "_plane", align_bytes=64)
+            nc.vector.quantize_mx(out=codes[:].bitcast(FP8X4), scales=plane[:], in_=bf[:].rearrange("p j t -> p (j t)"))
+            return codes, plane
+
+        wc_bf = keep.tile([P, R, PACK], BF16, name="wc_bf", align_bytes=64)
+        for h in range(2):
+            interleave(nc, wc_bf[:, h * HALF : (h + 1) * HALF, :], wc_raw[h][:])
+        wc_codes, wc_plane = quantize("wc", wc_bf, R)
+        picked = {}
+        for h in range(2):
+            for g in range(G):
+                words = keep.tile([P, HALF], U32, name="picked%d_%d" % (h, g), align_bytes=64)
+                col = (g * J + h * HALF) // 16
+                nc.vector.tensor_copy(words[:], table[:].bitcast(U32).indirect(offsets[:, col : col + HALF // 16]))
+                picked[h, g] = words
+
+        c_mx = []
+
+        def prepare_c(h):
+            bf = keep.tile([P, HALF, PACK], BF16, name="c_bf%d" % h, align_bytes=64)
+            interleave(nc, bf[:], c_raw[h][:])
+            c_mx.append(quantize("c%d" % h, bf, HALF))
+
+        def dealt(bank):
+            return bank[:].rearrange("j (p t) -> j t p", t=PACK)
+
+        def pool_chunk(u):
+            h, lo = divmod(u * CHUNK, HALF)
+            cols = slice(lo, lo + CHUNK)
+            banks = []
+            for g in range(G):
+                if g == 0:
+                    bank = psum.tile([P, R], F32, name="first_bank", bufs=2)
+                else:
+                    bank = psum.tile([P, R], F32, name="for_vector", bufs=3)
+                nc.tensor.matmul_mx(
+                    out=bank[:],
+                    lhsT=picked[h, g][:, cols].bitcast(FP8X4),
+                    lhsT_scale=picked_plane[:, g * J + u * CHUNK : g * J + (u + 1) * CHUNK],
+                    rhs=w_codes[:].bitcast(FP4X4),
+                    rhs_scale=w_plane[:],
+                    start=True,
+                    stop=True,
+                )
+                banks.append(bank)
+            first = staged[u // 2][:, u % 2, :, :]
+            nc.scalar.activation(out=first, in_=dealt(banks[0]), func=ACT.Copy)
+            second = work.tile([P, PACK, P], F32, name="second")
+            nc.vector.tensor_tensor(out=second[:], in0=dealt(banks[1]), in1=first, op=ALU.max)
+            pooled = work.tile([P, PACK, P], F32, name="pooled")
+            nc.vector.tensor_tensor(out=pooled[:], in0=dealt(banks[2]), in1=second[:], op=ALU.max)
+            return pooled
+
+        def own_chunk(u):
+            h, lo = divmod(u * CHUNK, HALF)
+            cols = slice(lo, lo + CHUNK)
+            own = psum.tile([P, R], F32, name="for_scalar", bufs=3)
+            nc.tensor.matmul_mx(
+                out=own[:],
+                lhsT=c_mx[h][0][:, cols].bitcast(FP8X4),
+                lhsT_scale=c_mx[h][1][:, cols],
+                rhs=wc_codes[:].bitcast(FP8X4),
+                rhs_scale=wc_plane[:],
+                start=True,
+                stop=True,
+            )
+            own_sb = staged[1][:, 2 + u, :, :]
+            nc.scalar.activation(out=own_sb, in_=dealt(own), func=ACT.Copy)
+            return own_sb
+
+        def hidden_chunk(pooled, own_sb):
+            total = psum.tile([P, PACK, CHUNK], F32, name="for_scalar", bufs=3)
+            for s, src in enumerate((own_sb, pooled)):
+                for t in range(PACK):
+                    nc.tensor.matmul(
+                        total[:, t, :],
+                        lhsT=src[:, t, :],
+                        rhs=ident[:],
+                        start=(s == 0 and t == 0),
+                        stop=(s == 1 and t == PACK - 1),
+                        is_transpose=True,
+                    )
+            h_bf = work.tile([P, CHUNK, PACK], BF16, name="h_bf", align_bytes=64)
+            nc.scalar.activation(out=h_bf[:], in_=total[:].rearrange("p t j -> p j t"), func=ACT.Relu)
+            h_codes = work.tile([P, CHUNK], U32, name="h_codes", align_bytes=64)
+            h_plane = work.tile([P, CHUNK], U8, name="h_plane", align_bytes=64)
+            nc.vector.quantize_mx(
+                out=h_codes[:].bitcast(FP8X4), scales=h_plane[:], in_=h_bf[:].rearrange("p j t -> p (j t)")
+            )
+            return h_codes, h_plane
+
+        def finish_chunk(u, h_codes, h_plane):
+            y = psum.tile([P, N // P, CHUNK], F32, name="for_vector", bufs=3)
+            for b in range(N // P):
+                nc.tensor.matmul_mx(
+                    out=y[:, b, :],
+                    lhsT=wd_codes[:, b * P : (b + 1) * P].bitcast(FP8X4),
+                    lhsT_scale=wd_plane[:, b * P : (b + 1) * P],
+                    rhs=h_codes[:].bitcast(FP8X4),
+                    rhs_scale=h_plane[:],
+                    start=True,
+                    stop=True,
+                )
+            cols = slice(u * CHUNK, (u + 1) * CHUNK)
+            result = work.tile([P, N // P, CHUNK], F32, name="result")
+            nc.vector.tensor_tensor(out=result[:], in0=y[:], in1=res_sb[u * CHUNK // HALF][:, :, u * CHUNK % HALF : u * CHUNK % HALF + CHUNK], op=ALU.add)
+            nc.sync.dma_start(out=out_rows[:, :, cols], in_=result[:])
+
+        staged = []
+        pooled = []
+        for h in range(2):
+            prepare_c(h)
+            staged.append(keep.tile([P, 2 + 4 * h, PACK, P], F32, name="staged", tag="c%d" % h))
+            if h == 0:
+                pooled.extend([pool_chunk(0), pool_chunk(1)])
+        pooled.append(pool_chunk(2))
+        own = [own_chunk(0)]
+        pooled.append(pool_chunk(3))
+        own.append(own_chunk(1))
+        hidden = [hidden_chunk(pooled[0], own[0])]
+        own.append(own_chunk(2))
+        hidden.append(hidden_chunk(pooled[1], own[1]))
+        own.append(own_chunk(3))
+        finish_chunk(0, *hidden[0])
+        hidden.append(hidden_chunk(pooled[2], own[2]))
+        finish_chunk(1, *hidden[1])
+        hidden.append(hidden_chunk(pooled[3], own[3]))
+        finish_chunk(2, *hidden[2])
+        finish_chunk(3, *hidden[3])

@@ -1,7 +1,6 @@
 from contextlib import ExitStack
 
 import concourse.mybir as mybir
-from concourse.masks import make_identity
 
 K, R, N, T, J = 512, 512, 512, 2048, 512
 G = 3
@@ -24,17 +23,9 @@ CHUNK = 128
 HALF = 256
 
 
-def load_plane(nc, plane, rows):
+def load_plane(queues, plane, rows):
     for q in range(4):
-        nc.sync.dma_start(out=plane[32 * q : 32 * q + 4, :].bitcast(I32), in_=rows[4 * q : 4 * q + 4, :].bitcast(I32))
-
-
-def interleave(nc, grouped, raw):
-    nc.scalar.activation(
-        out=grouped.rearrange("p (c i) t -> p c t i", i=4),
-        in_=raw.rearrange("p t (c i) -> p c t i", i=4),
-        func=ACT.Copy,
-    )
+        queues[q % len(queues)].dma_start(out=plane[32 * q : 32 * q + 4, :].bitcast(I32), in_=rows[4 * q : 4 * q + 4, :].bitcast(I32))
 
 
 def tile_list_pnet_res_kernel(
@@ -43,18 +34,15 @@ def tile_list_pnet_res_kernel(
     nc = tc.nc
     with ExitStack() as ctx:
         keep = ctx.enter_context(tc.tile_pool(name="keep", bufs=1))
-        work = ctx.enter_context(tc.tile_pool(name="work", bufs=4))
-        psum = ctx.enter_context(tc.psum_pool(name="psum", bufs=2))
+        psum = ctx.enter_context(tc.psum_pool(name="psum", bufs=4))
 
         offsets = keep.tile([P, G * J // 16], U16, name="offsets")
         tab_plane = keep.tile([P, T], U8, name="tab_plane", align_bytes=64)
-        w_plane = keep.tile([P, R], U8, name="w_plane", align_bytes=64)
+        w_plane_raw = keep.tile([P, R], U8, name="w_plane_raw", align_bytes=64)
         wd_plane = keep.tile([P, N], U8, name="wd_plane", align_bytes=64)
         nc.vector.memset(tab_plane[:].bitcast(I32), 0)
-        nc.vector.memset(w_plane[:].bitcast(I32), 0)
+        nc.vector.memset(w_plane_raw[:].bitcast(I32), 0)
         nc.vector.memset(wd_plane[:].bitcast(I32), 0)
-        ident = keep.tile([P, P], F32, name="ident")
-        make_identity(nc, ident[:])
 
         def load_half(name, rows, h):
             raw = keep.tile([P, PACK, HALF], F32, name="raw", tag="%s%d" % (name, h))
@@ -62,18 +50,19 @@ def tile_list_pnet_res_kernel(
             return raw
 
         nc.sync.dma_start(offsets[:], offs)
-        wc_raw = [load_half("wc", wc, 0)]
-        load_plane(nc, tab_plane, tab_scales[0])
-        wc_raw.append(load_half("wc", wc, 1))
-        w_codes = keep.tile([P, 2 * R], U8, name="w_codes", align_bytes=64)
-        nc.sync.dma_start(out=w_codes[:].bitcast(I32), in_=w_words[0].bitcast(I32))
+        w_raw = keep.tile([P, 2 * R], U8, name="w_raw", align_bytes=64)
+        nc.sync.dma_start(out=w_raw[:].bitcast(I32), in_=w_words[0].bitcast(I32))
         table = keep.tile([P, T], I32, name="table", align_bytes=64)
-        nc.sync.dma_start(out=table[:], in_=tab_words[0].rearrange("p t i -> p (t i)").bitcast(I32))
-        load_plane(nc, w_plane, w_scales[0])
+        table_rows = tab_words[0].rearrange("p t i -> p (t i)").bitcast(I32)
+        nc.sync.dma_start(out=table[:, 0 : T // 4], in_=table_rows[:, 0 : T // 4])
+        load_plane([nc.sync, nc.scalar], tab_plane, tab_scales[0])
+        nc.sync.dma_start(out=table[:, T // 4 : T], in_=table_rows[:, T // 4 : T])
+        load_plane([nc.sync], w_plane_raw, w_scales[0])
+        wc_raw = [load_half("wc", wc, h) for h in range(2)]
         c_raw = [load_half("c", c, h) for h in range(2)]
         wd_codes = keep.tile([P, N], I32, name="wd_codes", align_bytes=64)
         nc.sync.dma_start(out=wd_codes[:], in_=wd_words[0].rearrange("p n i -> p (n i)").bitcast(I32))
-        load_plane(nc, wd_plane, wd_scales[0])
+        load_plane([nc.sync], wd_plane, wd_scales[0])
         res_sb = []
         for h in range(2):
             rows = keep.tile([P, N // P, HALF], F32, name="res%d" % h)
@@ -81,137 +70,152 @@ def tile_list_pnet_res_kernel(
             res_sb.append(rows)
         out_rows = out.rearrange("(b p) j -> p b j", p=P)
 
+        w_codes = keep.tile([P, PACK, P], U16, name="w_codes", align_bytes=64)
+        nc.vector.tensor_copy(w_codes[:], w_raw[:].bitcast(U16).rearrange("p (m t) -> p t m", t=PACK))
+        w_plane = keep.tile([P, PACK, P], U8, name="w_plane", align_bytes=64)
+        nc.gpsimd.tensor_copy(w_plane[:], w_plane_raw[:].rearrange("p (m t) -> p t m", t=PACK))
+
         picked_plane = keep.tile([P, G * J], U8, name="picked_plane", align_bytes=64)
         nc.vector.tensor_copy(picked_plane[:], tab_plane[:].indirect(offsets[:]))
+        picked = keep.tile([P, G, J], U32, name="picked", align_bytes=64)
+        for g in range(G):
+            nc.vector.tensor_copy(
+                picked[:, g, :], table[:].bitcast(U32).indirect(offsets[:, g * J // 16 : (g + 1) * J // 16])
+            )
 
         def quantize(name, bf, width):
             codes = keep.tile([P, width], U32, name=name + "_codes", align_bytes=64)
             plane = keep.tile([P, width], U8, name=name + "_plane", align_bytes=64)
-            nc.vector.quantize_mx(out=codes[:].bitcast(FP8X4), scales=plane[:], in_=bf[:].rearrange("p j t -> p (j t)"))
+            nc.vector.quantize_mx(out=codes[:].bitcast(FP8X4), scales=plane[:], in_=bf)
             return codes, plane
 
-        wc_bf = keep.tile([P, R, PACK], BF16, name="wc_bf", align_bytes=64)
+        wc_bf = keep.tile([P, PACK, P, PACK], BF16, name="wc_bf", align_bytes=64)
         for h in range(2):
-            interleave(nc, wc_bf[:, h * HALF : (h + 1) * HALF, :], wc_raw[h][:])
-        wc_codes, wc_plane = quantize("wc", wc_bf, R)
-        picked = {}
-        for h in range(2):
-            for g in range(G):
-                words = keep.tile([P, HALF], U32, name="picked%d_%d" % (h, g), align_bytes=64)
-                col = (g * J + h * HALF) // 16
-                nc.vector.tensor_copy(words[:], table[:].bitcast(U32).indirect(offsets[:, col : col + HALF // 16]))
-                picked[h, g] = words
+            nc.scalar.activation(
+                out=wc_bf[:, :, h * HALF // PACK : (h + 1) * HALF // PACK, :].rearrange("p t m i -> p m i t"),
+                in_=wc_raw[h][:].rearrange("p i (m t) -> p m i t", t=PACK),
+                func=ACT.Copy,
+            )
+        wc_codes, wc_plane = quantize("wc", wc_bf[:].rearrange("p t m i -> p (t m i)"), R)
 
         c_mx = []
 
         def prepare_c(h):
-            bf = keep.tile([P, HALF, PACK], BF16, name="c_bf%d" % h, align_bytes=64)
-            interleave(nc, bf[:], c_raw[h][:])
-            c_mx.append(quantize("c%d" % h, bf, HALF))
-
-        def dealt(bank):
-            return bank[:].rearrange("j (p t) -> j t p", t=PACK)
-
-        def pool_chunk(u):
-            h, lo = divmod(u * CHUNK, HALF)
-            cols = slice(lo, lo + CHUNK)
-            banks = []
-            for g in range(G):
-                if g == 0:
-                    bank = psum.tile([P, R], F32, name="first_bank", bufs=2)
-                else:
-                    bank = psum.tile([P, R], F32, name="for_vector", bufs=3)
-                nc.tensor.matmul_mx(
-                    out=bank[:],
-                    lhsT=picked[h, g][:, cols].bitcast(FP8X4),
-                    lhsT_scale=picked_plane[:, g * J + u * CHUNK : g * J + (u + 1) * CHUNK],
-                    rhs=w_codes[:].bitcast(FP4X4),
-                    rhs_scale=w_plane[:],
-                    start=True,
-                    stop=True,
-                )
-                banks.append(bank)
-            first = staged[u // 2][:, u % 2, :, :]
-            nc.scalar.activation(out=first, in_=dealt(banks[0]), func=ACT.Copy)
-            second = work.tile([P, PACK, P], F32, name="second")
-            nc.vector.tensor_tensor(out=second[:], in0=dealt(banks[1]), in1=first, op=ALU.max)
-            pooled = work.tile([P, PACK, P], F32, name="pooled")
-            nc.vector.tensor_tensor(out=pooled[:], in0=dealt(banks[2]), in1=second[:], op=ALU.max)
-            return pooled
-
-        def own_chunk(u):
-            h, lo = divmod(u * CHUNK, HALF)
-            cols = slice(lo, lo + CHUNK)
-            own = psum.tile([P, R], F32, name="for_scalar", bufs=3)
-            nc.tensor.matmul_mx(
-                out=own[:],
-                lhsT=c_mx[h][0][:, cols].bitcast(FP8X4),
-                lhsT_scale=c_mx[h][1][:, cols],
-                rhs=wc_codes[:].bitcast(FP8X4),
-                rhs_scale=wc_plane[:],
-                start=True,
-                stop=True,
+            bf = keep.tile([P, HALF, PACK], BF16, name="c_bf", tag="c_bf%d" % h, align_bytes=64)
+            nc.scalar.activation(
+                out=bf[:].rearrange("p (c e) i -> p c i e", e=4),
+                in_=c_raw[h][:].rearrange("p i (c e) -> p c i e", e=4),
+                func=ACT.Copy,
             )
-            own_sb = staged[1][:, 2 + u, :, :]
-            nc.scalar.activation(out=own_sb, in_=dealt(own), func=ACT.Copy)
-            return own_sb
+            c_mx.append(quantize("c%d" % h, bf[:].rearrange("p j i -> p (j i)"), HALF))
 
-        def hidden_chunk(pooled, own_sb):
-            total = psum.tile([P, PACK, CHUNK], F32, name="for_scalar", bufs=3)
-            for s, src in enumerate((own_sb, pooled)):
-                for t in range(PACK):
-                    nc.tensor.matmul(
-                        total[:, t, :],
-                        lhsT=src[:, t, :],
-                        rhs=ident[:],
-                        start=(s == 0 and t == 0),
-                        stop=(s == 1 and t == PACK - 1),
-                        is_transpose=True,
+        def woven(bank):
+            return bank[:].rearrange("p t j -> p j t")
+
+        def project(u, g, with_own):
+            bank = psum.tile([P, PACK, CHUNK], F32, name="bank", tag="for_scalar" if g in (0, None) and (u, g) != (2, None) else "for_vector")
+            h, lo = divmod(u * CHUNK, HALF)
+            cols = slice(lo, lo + CHUNK)
+            for t in range(PACK):
+                if g is not None:
+                    nc.tensor.matmul_mx(
+                        out=bank[:, t, :],
+                        lhsT=w_codes[:, t, :].bitcast(FP4X4),
+                        lhsT_scale=w_plane[:, t, :],
+                        rhs=picked[:, g, u * CHUNK : (u + 1) * CHUNK].bitcast(FP8X4),
+                        rhs_scale=picked_plane[:, g * J + u * CHUNK : g * J + (u + 1) * CHUNK],
+                        start=True,
+                        stop=not with_own,
                     )
-            h_bf = work.tile([P, CHUNK, PACK], BF16, name="h_bf", align_bytes=64)
-            nc.scalar.activation(out=h_bf[:], in_=total[:].rearrange("p t j -> p j t"), func=ACT.Relu)
-            h_codes = work.tile([P, CHUNK], U32, name="h_codes", align_bytes=64)
-            h_plane = work.tile([P, CHUNK], U8, name="h_plane", align_bytes=64)
-            nc.vector.quantize_mx(
-                out=h_codes[:].bitcast(FP8X4), scales=h_plane[:], in_=h_bf[:].rearrange("p j t -> p (j t)")
+                if with_own:
+                    nc.tensor.matmul_mx(
+                        out=bank[:, t, :],
+                        lhsT=wc_codes[:, t * P : (t + 1) * P].bitcast(FP8X4),
+                        lhsT_scale=wc_plane[:, t * P : (t + 1) * P],
+                        rhs=c_mx[h][0][:, cols].bitcast(FP8X4),
+                        rhs_scale=c_mx[h][1][:, cols],
+                        start=g is None,
+                        stop=True,
+                    )
+            return bank
+
+        def first_max(u, first):
+            banks = [project(u, g, u == 3) for g in range(2)]
+            nc.scalar.activation(out=first, in_=woven(banks[0]), func=ACT.Copy)
+            second = keep.tile([P, CHUNK, PACK], F32, name="second%d" % u)
+            nc.vector.tensor_tensor(out=second[:], in0=woven(banks[1]), in1=first, op=ALU.max)
+            return second
+
+        def second_max(u, second, pooled):
+            bank = project(u, 2, False)
+            nc.vector.tensor_tensor(out=pooled, in0=woven(bank), in1=second[:], op=ALU.max)
+
+        def add_on_gpsimd(u, pooled, own):
+            bank = project(u, None, True)
+            nc.scalar.activation(out=own, in_=woven(bank), func=ACT.Copy)
+            total = keep.tile([P, CHUNK, PACK], F32, name="total%d" % u)
+            nc.gpsimd.tensor_tensor(out=total[:], in0=pooled, in1=own, op=ALU.add)
+            return total
+
+        def second_layer(name, h_bf, width):
+            h_codes, h_plane = quantize(name, h_bf[:].rearrange("p j t -> p (j t)"), width)
+            per_bank = 512 // width
+            banks = []
+            for b0 in range(0, N // P, per_bank):
+                y = psum.tile([P, per_bank, width], F32, name="y", tag="for_scalar")
+                for b in range(per_bank):
+                    rows = slice((b0 + b) * P, (b0 + b + 1) * P)
+                    nc.tensor.matmul_mx(
+                        out=y[:, b, :],
+                        lhsT=wd_codes[:, rows].bitcast(FP8X4),
+                        lhsT_scale=wd_plane[:, rows],
+                        rhs=h_codes[:].bitcast(FP8X4),
+                        rhs_scale=h_plane[:],
+                        start=True,
+                        stop=True,
+                    )
+                banks.append(y)
+            return banks
+
+        def finish(y, b0, blocks, lo, width):
+            half, at = divmod(lo, HALF)
+            result = keep.tile([P, blocks, width], F32, name="result_%d_%d" % (lo, b0))
+            nc.vector.tensor_tensor(
+                out=result[:], in0=y, in1=res_sb[half][:, b0 : b0 + blocks, at : at + width], op=ALU.add
             )
-            return h_codes, h_plane
+            nc.sync.dma_start(out=out_rows[:, b0 : b0 + blocks, lo : lo + width], in_=result[:])
 
-        def finish_chunk(u, h_codes, h_plane):
-            y = psum.tile([P, N // P, CHUNK], F32, name="for_vector", bufs=3)
-            for b in range(N // P):
-                nc.tensor.matmul_mx(
-                    out=y[:, b, :],
-                    lhsT=wd_codes[:, b * P : (b + 1) * P].bitcast(FP8X4),
-                    lhsT_scale=wd_plane[:, b * P : (b + 1) * P],
-                    rhs=h_codes[:].bitcast(FP8X4),
-                    rhs_scale=h_plane[:],
-                    start=True,
-                    stop=True,
-                )
-            cols = slice(u * CHUNK, (u + 1) * CHUNK)
-            result = work.tile([P, N // P, CHUNK], F32, name="result")
-            nc.vector.tensor_tensor(out=result[:], in0=y[:], in1=res_sb[u * CHUNK // HALF][:, :, u * CHUNK % HALF : u * CHUNK % HALF + CHUNK], op=ALU.add)
-            nc.sync.dma_start(out=out_rows[:, :, cols], in_=result[:])
+        h01 = keep.tile([P, HALF, PACK], BF16, name="h01", align_bytes=64)
+        h2 = keep.tile([P, CHUNK, PACK], BF16, name="h2", align_bytes=64)
+        h3 = keep.tile([P, CHUNK, PACK], BF16, name="h3", align_bytes=64)
 
-        staged = []
-        pooled = []
-        for h in range(2):
-            prepare_c(h)
-            staged.append(keep.tile([P, 2 + 4 * h, PACK, P], F32, name="staged", tag="c%d" % h))
-            if h == 0:
-                pooled.extend([pool_chunk(0), pool_chunk(1)])
-        pooled.append(pool_chunk(2))
-        own = [own_chunk(0)]
-        pooled.append(pool_chunk(3))
-        own.append(own_chunk(1))
-        hidden = [hidden_chunk(pooled[0], own[0])]
-        own.append(own_chunk(2))
-        hidden.append(hidden_chunk(pooled[1], own[1]))
-        own.append(own_chunk(3))
-        finish_chunk(0, *hidden[0])
-        hidden.append(hidden_chunk(pooled[2], own[2]))
-        finish_chunk(1, *hidden[1])
-        hidden.append(hidden_chunk(pooled[3], own[3]))
-        finish_chunk(2, *hidden[2])
-        finish_chunk(3, *hidden[3])
+        prepare_c(0)
+        early = keep.tile([P, 2, CHUNK, PACK], F32, name="early", tag="c0")
+        s0 = first_max(0, early[:, 0, :, :])
+        s1 = first_max(1, early[:, 1, :, :])
+        prepare_c(1)
+        late = keep.tile([P, 4, CHUNK, PACK], F32, name="late", tag="c1")
+        pooled = keep.tile([P, 3, CHUNK, PACK], F32, name="pooled", tag="c_bf1", align_bytes=64)
+        second_max(0, s0, pooled[:, 0, :, :])
+        s2 = first_max(2, late[:, 0, :, :])
+        t0 = add_on_gpsimd(0, pooled[:, 0, :, :], late[:, 1, :, :])
+        second_max(1, s1, pooled[:, 1, :, :])
+        t1 = add_on_gpsimd(1, pooled[:, 1, :, :], late[:, 2, :, :])
+        second_max(2, s2, pooled[:, 2, :, :])
+        s3 = first_max(3, late[:, 3, :, :])
+        nc.scalar.activation(out=h01[:, 0:CHUNK, :], in_=t0[:], func=ACT.Relu)
+        nc.scalar.activation(out=h01[:, CHUNK:HALF, :], in_=t1[:], func=ACT.Relu)
+        own2 = project(2, None, True)
+        t2 = keep.tile([P, CHUNK, PACK], F32, name="total2")
+        nc.vector.tensor_tensor(out=t2[:], in0=woven(own2), in1=pooled[:, 2, :, :], op=ALU.add)
+        nc.scalar.activation(out=h2[:], in_=t2[:], func=ACT.Relu)
+        last = project(3, 2, True)
+        y01 = second_layer("h01", h01, HALF)
+        nc.vector.scalar_tensor_tensor(out=h3[:], in0=woven(last), scalar=0.0, in1=s3[:], op0=ALU.max, op1=ALU.max)
+        y2 = second_layer("h2", h2, CHUNK)
+        finish(y01[0][:], 0, 2, 0, HALF)
+        y3 = second_layer("h3", h3, CHUNK)
+        finish(y01[1][:], 2, 2, 0, HALF)
+        finish(y2[0][:], 0, 4, 2 * CHUNK, CHUNK)
+        for b0 in (0, 2):
+            finish(y3[0][:, b0 : b0 + 2, :], b0, 2, 3 * CHUNK, CHUNK)

@@ -53,10 +53,8 @@ def tile_list_pnet_res_kernel(
         w_raw = keep.tile([P, 2 * R], U8, name="w_raw", align_bytes=64)
         nc.sync.dma_start(out=w_raw[:].bitcast(I32), in_=w_words[0].bitcast(I32))
         table = keep.tile([P, T], I32, name="table", align_bytes=64)
-        table_rows = tab_words[0].rearrange("p t i -> p (t i)").bitcast(I32)
-        nc.sync.dma_start(out=table[:, 0 : T // 4], in_=table_rows[:, 0 : T // 4])
-        load_plane([nc.sync, nc.scalar], tab_plane, tab_scales[0])
-        nc.sync.dma_start(out=table[:, T // 4 : T], in_=table_rows[:, T // 4 : T])
+        load_plane([nc.sync], tab_plane, tab_scales[0])
+        nc.sync.dma_start(out=table[:], in_=tab_words[0].rearrange("p t i -> p (t i)").bitcast(I32))
         load_plane([nc.sync], w_plane_raw, w_scales[0])
         wc_raw = [load_half("wc", wc, h) for h in range(2)]
         c_raw = [load_half("c", c, h) for h in range(2)]
@@ -116,27 +114,29 @@ def tile_list_pnet_res_kernel(
             bank = psum.tile([P, PACK, CHUNK], F32, name="bank", tag="for_scalar" if g in (0, None) and (u, g) != (2, None) else "for_vector")
             h, lo = divmod(u * CHUNK, HALF)
             cols = slice(lo, lo + CHUNK)
-            for t in range(PACK):
-                if g is not None:
-                    nc.tensor.matmul_mx(
-                        out=bank[:, t, :],
-                        lhsT=w_codes[:, t, :].bitcast(FP4X4),
-                        lhsT_scale=w_plane[:, t, :],
-                        rhs=picked[:, g, u * CHUNK : (u + 1) * CHUNK].bitcast(FP8X4),
-                        rhs_scale=picked_plane[:, g * J + u * CHUNK : g * J + (u + 1) * CHUNK],
-                        start=True,
-                        stop=not with_own,
-                    )
-                if with_own:
-                    nc.tensor.matmul_mx(
-                        out=bank[:, t, :],
-                        lhsT=wc_codes[:, t * P : (t + 1) * P].bitcast(FP8X4),
-                        lhsT_scale=wc_plane[:, t * P : (t + 1) * P],
-                        rhs=c_mx[h][0][:, cols].bitcast(FP8X4),
-                        rhs_scale=c_mx[h][1][:, cols],
-                        start=g is None,
-                        stop=True,
-                    )
+            passes = []
+            if g is not None:
+                moving = picked[:, g, u * CHUNK : (u + 1) * CHUNK].bitcast(FP8X4)
+                plane = picked_plane[:, g * J + u * CHUNK : g * J + (u + 1) * CHUNK]
+                passes.extend((t, w_codes[:, t, :].bitcast(FP4X4), w_plane[:, t, :], moving, plane) for t in range(PACK))
+            if with_own:
+                moving = c_mx[h][0][:, cols].bitcast(FP8X4)
+                plane = c_mx[h][1][:, cols]
+                passes.extend(
+                    (t, wc_codes[:, t * P : (t + 1) * P].bitcast(FP8X4), wc_plane[:, t * P : (t + 1) * P], moving, plane)
+                    for t in range(PACK)
+                )
+            one_group = len(passes) > PACK
+            for i, (t, lhs, lhs_plane, rhs, rhs_plane) in enumerate(passes):
+                nc.tensor.matmul_mx(
+                    out=bank[:, t, :],
+                    lhsT=lhs,
+                    lhsT_scale=lhs_plane,
+                    rhs=rhs,
+                    rhs_scale=rhs_plane,
+                    start=(i == 0 or not one_group),
+                    stop=(i == len(passes) - 1 or not one_group),
+                )
             return bank
 
         def first_max(u, first):

@@ -4,7 +4,7 @@ import concourse.mybir as mybir
 
 K, R, N, T, J = 512, 512, 512, 2048, 512
 G = 3
-FLOPS = 2 * 512 * 512 * 512 * 5
+FLOPS = 2 * J * (K * R * (G + 1) + R * N)
 
 F32 = mybir.dt.float32
 BF16 = mybir.dt.bfloat16
@@ -19,13 +19,20 @@ ALU = mybir.AluOpType
 
 P = 128
 PACK = 4
+PER_COLUMN = 16
+LINE = 4
 CHUNK = 128
 HALF = 256
+BLOCKS_PER_BANK = 2
+BANKS_PER_READER = 4
 
 
-def load_plane(queues, plane, rows):
-    for q in range(4):
-        queues[q % len(queues)].dma_start(out=plane[32 * q : 32 * q + 4, :].bitcast(I32), in_=rows[4 * q : 4 * q + 4, :].bitcast(I32))
+def load_plane(nc, plane, rows):
+    for quadrant in range(4):
+        nc.sync.dma_start(
+            out=plane[32 * quadrant : 32 * quadrant + 4, :].bitcast(I32),
+            in_=rows[4 * quadrant : 4 * quadrant + 4, :].bitcast(I32),
+        )
 
 
 def tile_list_pnet_res_kernel(
@@ -34,39 +41,40 @@ def tile_list_pnet_res_kernel(
     nc = tc.nc
     with ExitStack() as ctx:
         keep = ctx.enter_context(tc.tile_pool(name="keep", bufs=1))
-        psum = ctx.enter_context(tc.psum_pool(name="psum", bufs=4))
+        psum = ctx.enter_context(tc.psum_pool(name="psum", bufs=BANKS_PER_READER))
 
-        offsets = keep.tile([P, G * J // 16], U16, name="offsets")
+        offsets = keep.tile([P, G * J // PER_COLUMN], U16, name="offsets")
         tab_plane = keep.tile([P, T], U8, name="tab_plane", align_bytes=64)
         w_plane_raw = keep.tile([P, R], U8, name="w_plane_raw", align_bytes=64)
         wd_plane = keep.tile([P, N], U8, name="wd_plane", align_bytes=64)
-        nc.vector.memset(tab_plane[:].bitcast(I32), 0)
-        nc.vector.memset(w_plane_raw[:].bitcast(I32), 0)
-        nc.vector.memset(wd_plane[:].bitcast(I32), 0)
+        for plane in (tab_plane, w_plane_raw, wd_plane):
+            nc.vector.memset(plane[:].bitcast(I32), 0)
 
-        def load_half(name, rows, h):
-            raw = keep.tile([P, PACK, HALF], F32, name="raw", tag="%s%d" % (name, h))
-            nc.sync.dma_start(out=raw[:], in_=rows.rearrange("(p t) r -> p t r", t=PACK)[:, :, h * HALF : (h + 1) * HALF])
+        def load_half(name, rows, half):
+            raw = keep.tile([P, PACK, HALF], F32, name="raw", tag="%s%d" % (name, half))
+            view = rows.rearrange("(p i) x -> p i x", i=PACK)
+            nc.sync.dma_start(out=raw[:], in_=view[:, :, half * HALF : (half + 1) * HALF])
             return raw
 
         nc.sync.dma_start(offsets[:], offs)
         w_raw = keep.tile([P, 2 * R], U8, name="w_raw", align_bytes=64)
         nc.sync.dma_start(out=w_raw[:].bitcast(I32), in_=w_words[0].bitcast(I32))
         table = keep.tile([P, T], I32, name="table", align_bytes=64)
-        load_plane([nc.sync], tab_plane, tab_scales[0])
+        load_plane(nc, tab_plane, tab_scales[0])
         nc.sync.dma_start(out=table[:], in_=tab_words[0].rearrange("p t i -> p (t i)").bitcast(I32))
-        load_plane([nc.sync], w_plane_raw, w_scales[0])
-        wc_raw = [load_half("wc", wc, h) for h in range(2)]
-        c_raw = [load_half("c", c, h) for h in range(2)]
+        load_plane(nc, w_plane_raw, w_scales[0])
+        wc_raw = [load_half("wc", wc, half) for half in range(2)]
+        c_raw = [load_half("c", c, half) for half in range(2)]
         wd_codes = keep.tile([P, N], I32, name="wd_codes", align_bytes=64)
         nc.sync.dma_start(out=wd_codes[:], in_=wd_words[0].rearrange("p n i -> p (n i)").bitcast(I32))
-        load_plane([nc.sync], wd_plane, wd_scales[0])
-        res_sb = []
-        for h in range(2):
-            rows = keep.tile([P, N // P, HALF], F32, name="res%d" % h)
-            nc.sync.dma_start(out=rows[:], in_=res.rearrange("(b p) j -> p b j", p=P)[:, :, h * HALF : (h + 1) * HALF])
-            res_sb.append(rows)
+        load_plane(nc, wd_plane, wd_scales[0])
+        res_rows = res.rearrange("(b p) j -> p b j", p=P)
         out_rows = out.rearrange("(b p) j -> p b j", p=P)
+        res_sb = []
+        for half in range(2):
+            rows = keep.tile([P, N // P, HALF], F32, name="res%d" % half)
+            nc.sync.dma_start(out=rows[:], in_=res_rows[:, :, half * HALF : (half + 1) * HALF])
+            res_sb.append(rows)
 
         w_codes = keep.tile([P, PACK, P], U16, name="w_codes", align_bytes=64)
         nc.vector.tensor_copy(w_codes[:], w_raw[:].bitcast(U16).rearrange("p (m t) -> p t m", t=PACK))
@@ -77,94 +85,100 @@ def tile_list_pnet_res_kernel(
         nc.vector.tensor_copy(picked_plane[:], tab_plane[:].indirect(offsets[:]))
         picked = keep.tile([P, G, J], U32, name="picked", align_bytes=64)
         for g in range(G):
-            nc.vector.tensor_copy(
-                picked[:, g, :], table[:].bitcast(U32).indirect(offsets[:, g * J // 16 : (g + 1) * J // 16])
-            )
+            entries = offsets[:, g * J // PER_COLUMN : (g + 1) * J // PER_COLUMN]
+            nc.vector.tensor_copy(picked[:, g, :], table[:].bitcast(U32).indirect(entries))
 
-        def quantize(name, bf, width):
+        def quantize(name, values, width):
             codes = keep.tile([P, width], U32, name=name + "_codes", align_bytes=64)
-            plane = keep.tile([P, width], U8, name=name + "_plane", align_bytes=64)
-            nc.vector.quantize_mx(out=codes[:].bitcast(FP8X4), scales=plane[:], in_=bf)
-            return codes, plane
+            scales = keep.tile([P, width], U8, name=name + "_plane", align_bytes=64)
+            nc.vector.quantize_mx(out=codes[:].bitcast(FP8X4), scales=scales[:], in_=values)
+            return codes, scales
 
         wc_bf = keep.tile([P, PACK, P, PACK], BF16, name="wc_bf", align_bytes=64)
-        for h in range(2):
+        for half in range(2):
+            dealt = wc_bf[:, :, half * HALF // PACK : (half + 1) * HALF // PACK, :]
             nc.scalar.activation(
-                out=wc_bf[:, :, h * HALF // PACK : (h + 1) * HALF // PACK, :].rearrange("p t m i -> p m i t"),
-                in_=wc_raw[h][:].rearrange("p i (m t) -> p m i t", t=PACK),
+                out=dealt.rearrange("p t m i -> p m i t"),
+                in_=wc_raw[half][:].rearrange("p i (m t) -> p m i t", t=PACK),
                 func=ACT.Copy,
             )
         wc_codes, wc_plane = quantize("wc", wc_bf[:].rearrange("p t m i -> p (t m i)"), R)
 
         c_mx = []
 
-        def prepare_c(h):
-            bf = keep.tile([P, HALF, PACK], BF16, name="c_bf", tag="c_bf%d" % h, align_bytes=64)
+        def prepare_c(half):
+            c_bf = keep.tile([P, HALF, PACK], BF16, name="c_bf", tag="c_bf%d" % half, align_bytes=64)
             nc.scalar.activation(
-                out=bf[:].rearrange("p (c e) i -> p c i e", e=4),
-                in_=c_raw[h][:].rearrange("p i (c e) -> p c i e", e=4),
+                out=c_bf[:].rearrange("p (x e) i -> p x i e", e=LINE),
+                in_=c_raw[half][:].rearrange("p i (x e) -> p x i e", e=LINE),
                 func=ACT.Copy,
             )
-            c_mx.append(quantize("c%d" % h, bf[:].rearrange("p j i -> p (j i)"), HALF))
+            c_mx.append(quantize("c%d" % half, c_bf[:].rearrange("p j i -> p (j i)"), HALF))
 
-        def woven(bank):
+        def by_point(bank):
             return bank[:].rearrange("p t j -> p j t")
 
-        def project(u, g, with_own):
-            bank = psum.tile([P, PACK, CHUNK], F32, name="bank", tag="for_scalar" if g in (0, None) and (u, g) != (2, None) else "for_vector")
-            h, lo = divmod(u * CHUNK, HALF)
-            cols = slice(lo, lo + CHUNK)
+        def project(u, tag, g=None, own=False):
+            bank = psum.tile([P, PACK, CHUNK], F32, name="bank", tag=tag)
             passes = []
             if g is not None:
                 moving = picked[:, g, u * CHUNK : (u + 1) * CHUNK].bitcast(FP8X4)
-                plane = picked_plane[:, g * J + u * CHUNK : g * J + (u + 1) * CHUNK]
-                passes.extend((t, w_codes[:, t, :].bitcast(FP4X4), w_plane[:, t, :], moving, plane) for t in range(PACK))
-            if with_own:
-                moving = c_mx[h][0][:, cols].bitcast(FP8X4)
-                plane = c_mx[h][1][:, cols]
-                passes.extend(
-                    (t, wc_codes[:, t * P : (t + 1) * P].bitcast(FP8X4), wc_plane[:, t * P : (t + 1) * P], moving, plane)
-                    for t in range(PACK)
-                )
-            one_group = len(passes) > PACK
-            for i, (t, lhs, lhs_plane, rhs, rhs_plane) in enumerate(passes):
+                scales = picked_plane[:, g * J + u * CHUNK : g * J + (u + 1) * CHUNK]
+                for t in range(PACK):
+                    passes.append((t, w_codes[:, t, :].bitcast(FP4X4), w_plane[:, t, :], moving, scales))
+            if own:
+                half, start = divmod(u * CHUNK, HALF)
+                c_codes, c_plane = c_mx[half]
+                moving = c_codes[:, start : start + CHUNK].bitcast(FP8X4)
+                scales = c_plane[:, start : start + CHUNK]
+                for t in range(PACK):
+                    run = slice(t * P, (t + 1) * P)
+                    passes.append((t, wc_codes[:, run].bitcast(FP8X4), wc_plane[:, run], moving, scales))
+            lone = len(passes) == PACK
+            for number, (t, lhs, lhs_scales, rhs, rhs_scales) in enumerate(passes):
                 nc.tensor.matmul_mx(
                     out=bank[:, t, :],
                     lhsT=lhs,
-                    lhsT_scale=lhs_plane,
+                    lhsT_scale=lhs_scales,
                     rhs=rhs,
-                    rhs_scale=rhs_plane,
-                    start=(i == 0 or not one_group),
-                    stop=(i == len(passes) - 1 or not one_group),
+                    rhs_scale=rhs_scales,
+                    start=lone or number == 0,
+                    stop=lone or number == len(passes) - 1,
                 )
             return bank
 
-        def first_max(u, first):
-            banks = [project(u, g, u == 3) for g in range(2)]
-            nc.scalar.activation(out=first, in_=woven(banks[0]), func=ACT.Copy)
-            second = keep.tile([P, CHUNK, PACK], F32, name="second%d" % u)
-            nc.vector.tensor_tensor(out=second[:], in0=woven(banks[1]), in1=first, op=ALU.max)
-            return second
+        def first_max(u, copy_of_a0, own=False):
+            a0 = project(u, "first_layer_scalar", g=0, own=own)
+            a1 = project(u, "first_layer_vector", g=1, own=own)
+            nc.scalar.activation(out=copy_of_a0, in_=by_point(a0), func=ACT.Copy)
+            partial = keep.tile([P, CHUNK, PACK], F32, name="partial%d" % u)
+            nc.vector.tensor_tensor(out=partial[:], in0=by_point(a1), in1=copy_of_a0, op=ALU.max)
+            return partial
 
-        def second_max(u, second, pooled):
-            bank = project(u, 2, False)
-            nc.vector.tensor_tensor(out=pooled, in0=woven(bank), in1=second[:], op=ALU.max)
+        def second_max(u, partial, pooled):
+            a2 = project(u, "first_layer_vector", g=2)
+            nc.vector.tensor_tensor(out=pooled, in0=by_point(a2), in1=partial[:], op=ALU.max)
 
-        def add_on_gpsimd(u, pooled, own):
-            bank = project(u, None, True)
-            nc.scalar.activation(out=own, in_=woven(bank), func=ACT.Copy)
+        def add_own_on_gpsimd(u, pooled, copy_of_own):
+            bank = project(u, "first_layer_scalar", own=True)
+            nc.scalar.activation(out=copy_of_own, in_=by_point(bank), func=ACT.Copy)
             total = keep.tile([P, CHUNK, PACK], F32, name="total%d" % u)
-            nc.gpsimd.tensor_tensor(out=total[:], in0=pooled, in1=own, op=ALU.add)
+            nc.gpsimd.tensor_tensor(out=total[:], in0=pooled, in1=copy_of_own, op=ALU.add)
             return total
 
-        def second_layer(name, h_bf, width):
-            h_codes, h_plane = quantize(name, h_bf[:].rearrange("p j t -> p (j t)"), width)
-            per_bank = 512 // width
+        def add_own_on_vector(u, pooled):
+            bank = project(u, "first_layer_vector", own=True)
+            total = keep.tile([P, CHUNK, PACK], F32, name="total%d" % u)
+            nc.vector.tensor_tensor(out=total[:], in0=by_point(bank), in1=pooled, op=ALU.add)
+            return total
+
+        def second_layer(half):
+            h_codes, h_plane = quantize("h%d" % half, h_bf[half][:].rearrange("p j t -> p (j t)"), HALF)
             banks = []
-            for b0 in range(0, N // P, per_bank):
-                y = psum.tile([P, per_bank, width], F32, name="y", tag="for_scalar")
-                for b in range(per_bank):
-                    rows = slice((b0 + b) * P, (b0 + b + 1) * P)
+            for first_block in range(0, N // P, BLOCKS_PER_BANK):
+                y = psum.tile([P, BLOCKS_PER_BANK, HALF], F32, name="y", tag="first_layer_scalar")
+                for b in range(BLOCKS_PER_BANK):
+                    rows = slice((first_block + b) * P, (first_block + b + 1) * P)
                     nc.tensor.matmul_mx(
                         out=y[:, b, :],
                         lhsT=wd_codes[:, rows].bitcast(FP8X4),
@@ -177,45 +191,53 @@ def tile_list_pnet_res_kernel(
                 banks.append(y)
             return banks
 
-        def finish(y, b0, blocks, lo, width):
-            half, at = divmod(lo, HALF)
-            result = keep.tile([P, blocks, width], F32, name="result_%d_%d" % (lo, b0))
-            nc.vector.tensor_tensor(
-                out=result[:], in0=y, in1=res_sb[half][:, b0 : b0 + blocks, at : at + width], op=ALU.add
-            )
-            nc.sync.dma_start(out=out_rows[:, b0 : b0 + blocks, lo : lo + width], in_=result[:])
+        def finish(half, banks, bank_number, step):
+            for b in range(0, BLOCKS_PER_BANK, step):
+                block = bank_number * BLOCKS_PER_BANK + b
+                result = keep.tile([P, step, HALF], F32, name="result%d_%d" % (half, block))
+                nc.vector.tensor_tensor(
+                    out=result[:],
+                    in0=banks[bank_number][:, b : b + step, :],
+                    in1=res_sb[half][:, block : block + step, :],
+                    op=ALU.add,
+                )
+                nc.sync.dma_start(
+                    out=out_rows[:, block : block + step, half * HALF : (half + 1) * HALF], in_=result[:]
+                )
 
-        h01 = keep.tile([P, HALF, PACK], BF16, name="h01", align_bytes=64)
-        h2 = keep.tile([P, CHUNK, PACK], BF16, name="h2", align_bytes=64)
-        h3 = keep.tile([P, CHUNK, PACK], BF16, name="h3", align_bytes=64)
+        h_bf = [keep.tile([P, HALF, PACK], BF16, name="h_bf%d" % half, align_bytes=64) for half in range(2)]
+
+        def h_chunk(u):
+            half, start = divmod(u * CHUNK, HALF)
+            return h_bf[half][:, start : start + CHUNK, :]
 
         prepare_c(0)
         early = keep.tile([P, 2, CHUNK, PACK], F32, name="early", tag="c0")
-        s0 = first_max(0, early[:, 0, :, :])
-        s1 = first_max(1, early[:, 1, :, :])
+        partial0 = first_max(0, early[:, 0, :, :])
+        partial1 = first_max(1, early[:, 1, :, :])
         prepare_c(1)
         late = keep.tile([P, 4, CHUNK, PACK], F32, name="late", tag="c1")
         pooled = keep.tile([P, 3, CHUNK, PACK], F32, name="pooled", tag="c_bf1", align_bytes=64)
-        second_max(0, s0, pooled[:, 0, :, :])
-        s2 = first_max(2, late[:, 0, :, :])
-        t0 = add_on_gpsimd(0, pooled[:, 0, :, :], late[:, 1, :, :])
-        second_max(1, s1, pooled[:, 1, :, :])
-        t1 = add_on_gpsimd(1, pooled[:, 1, :, :], late[:, 2, :, :])
-        second_max(2, s2, pooled[:, 2, :, :])
-        s3 = first_max(3, late[:, 3, :, :])
-        nc.scalar.activation(out=h01[:, 0:CHUNK, :], in_=t0[:], func=ACT.Relu)
-        nc.scalar.activation(out=h01[:, CHUNK:HALF, :], in_=t1[:], func=ACT.Relu)
-        own2 = project(2, None, True)
-        t2 = keep.tile([P, CHUNK, PACK], F32, name="total2")
-        nc.vector.tensor_tensor(out=t2[:], in0=woven(own2), in1=pooled[:, 2, :, :], op=ALU.add)
-        nc.scalar.activation(out=h2[:], in_=t2[:], func=ACT.Relu)
-        last = project(3, 2, True)
-        y01 = second_layer("h01", h01, HALF)
-        nc.vector.scalar_tensor_tensor(out=h3[:], in0=woven(last), scalar=0.0, in1=s3[:], op0=ALU.max, op1=ALU.max)
-        y2 = second_layer("h2", h2, CHUNK)
-        finish(y01[0][:], 0, 2, 0, HALF)
-        y3 = second_layer("h3", h3, CHUNK)
-        finish(y01[1][:], 2, 2, 0, HALF)
-        finish(y2[0][:], 0, 4, 2 * CHUNK, CHUNK)
-        for b0 in (0, 2):
-            finish(y3[0][:, b0 : b0 + 2, :], b0, 2, 3 * CHUNK, CHUNK)
+
+        second_max(0, partial0, pooled[:, 0, :, :])
+        partial2 = first_max(2, late[:, 0, :, :])
+        total0 = add_own_on_gpsimd(0, pooled[:, 0, :, :], late[:, 1, :, :])
+        second_max(1, partial1, pooled[:, 1, :, :])
+        total1 = add_own_on_gpsimd(1, pooled[:, 1, :, :], late[:, 2, :, :])
+        second_max(2, partial2, pooled[:, 2, :, :])
+        partial3 = first_max(3, late[:, 3, :, :], own=True)
+        nc.scalar.activation(out=h_chunk(0), in_=total0[:], func=ACT.Relu)
+        nc.scalar.activation(out=h_chunk(1), in_=total1[:], func=ACT.Relu)
+        total2 = add_own_on_vector(2, pooled[:, 2, :, :])
+        nc.scalar.activation(out=h_chunk(2), in_=total2[:], func=ACT.Relu)
+        last = project(3, "first_layer_vector", g=2, own=True)
+        y0 = second_layer(0)
+        nc.vector.scalar_tensor_tensor(
+            out=h_chunk(3), in0=by_point(last), scalar=0.0, in1=partial3[:], op0=ALU.max, op1=ALU.max
+        )
+
+        finish(0, y0, 0, step=1)
+        y1 = second_layer(1)
+        finish(0, y0, 1, step=BLOCKS_PER_BANK)
+        finish(1, y1, 0, step=BLOCKS_PER_BANK)
+        finish(1, y1, 1, step=1)

@@ -24,7 +24,6 @@ LINE = 4
 CHUNK = 128
 HALF = 256
 BLOCKS_PER_BANK = 2
-BANKS_PER_READER = 4
 
 
 def load_plane(nc, plane, rows):
@@ -41,7 +40,7 @@ def tile_list_pnet_res_kernel(
     nc = tc.nc
     with ExitStack() as ctx:
         keep = ctx.enter_context(tc.tile_pool(name="keep", bufs=1))
-        psum = ctx.enter_context(tc.psum_pool(name="psum", bufs=BANKS_PER_READER))
+        psum = ctx.enter_context(tc.psum_pool(name="psum", bufs=1))
 
         offsets = keep.tile([P, G * J // PER_COLUMN], U16, name="offsets")
         tab_plane = keep.tile([P, T], U8, name="tab_plane", align_bytes=64)
@@ -51,7 +50,7 @@ def tile_list_pnet_res_kernel(
             nc.vector.memset(plane[:].bitcast(I32), 0)
 
         def load_half(name, rows, half):
-            raw = keep.tile([P, PACK, HALF], F32, name="raw", tag="%s%d" % (name, half))
+            raw = keep.tile([P, PACK, HALF], F32, name="raw", tag="%s%d" % (name, half), align_bytes=64)
             view = rows.rearrange("(p i) x -> p i x", i=PACK)
             nc.sync.dma_start(out=raw[:], in_=view[:, :, half * HALF : (half + 1) * HALF])
             return raw
@@ -83,13 +82,16 @@ def tile_list_pnet_res_kernel(
 
         picked_plane = keep.tile([P, G * J], U8, name="picked_plane", align_bytes=64)
         nc.vector.tensor_copy(picked_plane[:], tab_plane[:].indirect(offsets[:]))
-        picked = keep.tile([P, G, J], U32, name="picked", align_bytes=64)
-        for g in range(G):
-            entries = offsets[:, g * J // PER_COLUMN : (g + 1) * J // PER_COLUMN]
-            nc.vector.tensor_copy(picked[:, g, :], table[:].bitcast(U32).indirect(entries))
+        picked = {}
+        for g, first, count, tag in ((0, 0, HALF, "c_bf1"), (0, HALF, HALF, "g0"), (1, 0, J, "g1"), (2, 0, J, "g2")):
+            words = keep.tile([P, count], U32, name="picked", tag=tag, align_bytes=64)
+            entries = offsets[:, (g * J + first) // PER_COLUMN : (g * J + first + count) // PER_COLUMN]
+            nc.vector.tensor_copy(words[:], table[:].bitcast(U32).indirect(entries))
+            for start in range(0, count, CHUNK):
+                picked[g, (first + start) // CHUNK] = words[:, start : start + CHUNK]
 
-        def quantize(name, values, width):
-            codes = keep.tile([P, width], U32, name=name + "_codes", align_bytes=64)
+        def quantize(name, values, width, tag=None):
+            codes = keep.tile([P, width], U32, name=name + "_codes", tag=tag or name + "_codes", align_bytes=64)
             scales = keep.tile([P, width], U8, name=name + "_plane", align_bytes=64)
             nc.vector.quantize_mx(out=codes[:].bitcast(FP8X4), scales=scales[:], in_=values)
             return codes, scales
@@ -106,23 +108,25 @@ def tile_list_pnet_res_kernel(
 
         c_mx = []
 
-        def prepare_c(half):
+        def prepare_c(half, tag=None):
             c_bf = keep.tile([P, HALF, PACK], BF16, name="c_bf", tag="c_bf%d" % half, align_bytes=64)
-            nc.scalar.activation(
-                out=c_bf[:].rearrange("p (x e) i -> p x i e", e=LINE),
-                in_=c_raw[half][:].rearrange("p i (x e) -> p x i e", e=LINE),
-                func=ACT.Copy,
-            )
-            c_mx.append(quantize("c%d" % half, c_bf[:].rearrange("p j i -> p (j i)"), HALF))
+            if half == 0:
+                rows = c_raw[half][:].rearrange("p i j -> p j i")
+                nc.gpsimd.tensor_scalar(out=c_bf[:], in0=rows, scalar1=1.0, scalar2=0.0, op0=ALU.mult, op1=ALU.add)
+            else:
+                woven = c_bf[:].rearrange("p (x e) i -> p x i e", e=LINE)
+                rows = c_raw[half][:].rearrange("p i (x e) -> p x i e", e=LINE)
+                nc.scalar.activation(out=woven, in_=rows, func=ACT.Copy)
+            c_mx.append(quantize("c%d" % half, c_bf[:].rearrange("p j i -> p (j i)"), HALF, tag))
 
         def by_point(bank):
             return bank[:].rearrange("p t j -> p j t")
 
-        def project(u, tag, g=None, own=False):
-            bank = psum.tile([P, PACK, CHUNK], F32, name="bank", tag=tag)
+        def project(u, bank_number, g=None, own=False):
+            bank = psum.tile([P, PACK, CHUNK], F32, name="bank", tag="bank%d" % bank_number)
             passes = []
             if g is not None:
-                moving = picked[:, g, u * CHUNK : (u + 1) * CHUNK].bitcast(FP8X4)
+                moving = picked[g, u].bitcast(FP8X4)
                 scales = picked_plane[:, g * J + u * CHUNK : g * J + (u + 1) * CHUNK]
                 for t in range(PACK):
                     passes.append((t, w_codes[:, t, :].bitcast(FP4X4), w_plane[:, t, :], moving, scales))
@@ -147,36 +151,17 @@ def tile_list_pnet_res_kernel(
                 )
             return bank
 
-        def first_max(u, copy_of_a0, own=False):
-            a0 = project(u, "first_layer_scalar", g=0, own=own)
-            a1 = project(u, "first_layer_vector", g=1, own=own)
-            nc.scalar.activation(out=copy_of_a0, in_=by_point(a0), func=ACT.Copy)
-            partial = keep.tile([P, CHUNK, PACK], F32, name="partial%d" % u)
-            nc.vector.tensor_tensor(out=partial[:], in0=by_point(a1), in1=copy_of_a0, op=ALU.max)
-            return partial
+        def copy_out(bank, copy):
+            nc.scalar.activation(out=copy, in_=by_point(bank), func=ACT.Copy)
 
-        def second_max(u, partial, pooled):
-            a2 = project(u, "first_layer_vector", g=2)
-            nc.vector.tensor_tensor(out=pooled, in0=by_point(a2), in1=partial[:], op=ALU.max)
+        def combine(result, bank, other, op):
+            nc.vector.tensor_tensor(out=result, in0=by_point(bank), in1=other, op=op)
 
-        def add_own_on_gpsimd(u, pooled, copy_of_own):
-            bank = project(u, "first_layer_scalar", own=True)
-            nc.scalar.activation(out=copy_of_own, in_=by_point(bank), func=ACT.Copy)
-            total = keep.tile([P, CHUNK, PACK], F32, name="total%d" % u)
-            nc.gpsimd.tensor_tensor(out=total[:], in0=pooled, in1=copy_of_own, op=ALU.add)
-            return total
-
-        def add_own_on_vector(u, pooled):
-            bank = project(u, "first_layer_vector", own=True)
-            total = keep.tile([P, CHUNK, PACK], F32, name="total%d" % u)
-            nc.vector.tensor_tensor(out=total[:], in0=by_point(bank), in1=pooled, op=ALU.add)
-            return total
-
-        def second_layer(half):
+        def second_layer(half, bank_numbers):
             h_codes, h_plane = quantize("h%d" % half, h_bf[half][:].rearrange("p j t -> p (j t)"), HALF)
             banks = []
-            for first_block in range(0, N // P, BLOCKS_PER_BANK):
-                y = psum.tile([P, BLOCKS_PER_BANK, HALF], F32, name="y", tag="first_layer_scalar")
+            for number, first_block in zip(bank_numbers, range(0, N // P, BLOCKS_PER_BANK)):
+                y = psum.tile([P, BLOCKS_PER_BANK, HALF], F32, name="y", tag="bank%d" % number)
                 for b in range(BLOCKS_PER_BANK):
                     rows = slice((first_block + b) * P, (first_block + b + 1) * P)
                     nc.tensor.matmul_mx(
@@ -191,16 +176,18 @@ def tile_list_pnet_res_kernel(
                 banks.append(y)
             return banks
 
-        def finish(half, banks, bank_number, step):
+        def finish(half, banks, bank_number, step, on_gpsimd=False):
             for b in range(0, BLOCKS_PER_BANK, step):
                 block = bank_number * BLOCKS_PER_BANK + b
                 result = keep.tile([P, step, HALF], F32, name="result%d_%d" % (half, block))
-                nc.vector.tensor_tensor(
-                    out=result[:],
-                    in0=banks[bank_number][:, b : b + step, :],
-                    in1=res_sb[half][:, block : block + step, :],
-                    op=ALU.add,
-                )
+                y = banks[bank_number][:, b : b + step, :]
+                residual = res_sb[half][:, block : block + step, :]
+                if on_gpsimd:
+                    copy = keep.tile([P, step, HALF], F32, name="y_copy%d_%d" % (half, block))
+                    nc.scalar.activation(out=copy[:], in_=y, func=ACT.Copy)
+                    nc.gpsimd.tensor_tensor(out=result[:], in0=copy[:], in1=residual, op=ALU.add)
+                else:
+                    nc.vector.tensor_tensor(out=result[:], in0=y, in1=residual, op=ALU.add)
                 nc.sync.dma_start(
                     out=out_rows[:, block : block + step, half * HALF : (half + 1) * HALF], in_=result[:]
                 )
@@ -212,32 +199,51 @@ def tile_list_pnet_res_kernel(
             return h_bf[half][:, start : start + CHUNK, :]
 
         prepare_c(0)
-        early = keep.tile([P, 2, CHUNK, PACK], F32, name="early", tag="c0")
-        partial0 = first_max(0, early[:, 0, :, :])
-        partial1 = first_max(1, early[:, 1, :, :])
-        prepare_c(1)
-        late = keep.tile([P, 4, CHUNK, PACK], F32, name="late", tag="c1")
-        pooled = keep.tile([P, 3, CHUNK, PACK], F32, name="pooled", tag="c_bf1", align_bytes=64)
-
-        second_max(0, partial0, pooled[:, 0, :, :])
-        partial2 = first_max(2, late[:, 0, :, :])
-        total0 = add_own_on_gpsimd(0, pooled[:, 0, :, :], late[:, 1, :, :])
-        second_max(1, partial1, pooled[:, 1, :, :])
-        total1 = add_own_on_gpsimd(1, pooled[:, 1, :, :], late[:, 2, :, :])
-        second_max(2, partial2, pooled[:, 2, :, :])
-        partial3 = first_max(3, late[:, 3, :, :], own=True)
-        nc.scalar.activation(out=h_chunk(0), in_=total0[:], func=ACT.Relu)
-        nc.scalar.activation(out=h_chunk(1), in_=total1[:], func=ACT.Relu)
-        total2 = add_own_on_vector(2, pooled[:, 2, :, :])
-        nc.scalar.activation(out=h_chunk(2), in_=total2[:], func=ACT.Relu)
-        last = project(3, "first_layer_vector", g=2, own=True)
-        y0 = second_layer(0)
+        first_copy = keep.tile([P, CHUNK, PACK], F32, name="first_copy", tag="wc1", align_bytes=64)
+        next_copies = keep.tile([P, 2, CHUNK, PACK], F32, name="next_copies", tag="wc0", align_bytes=64)
+        a0_copy = [first_copy[:], next_copies[:, 0], next_copies[:, 1]]
+        early = keep.tile([P, 2, CHUNK, PACK], F32, name="early", tag="c0", align_bytes=64)
+        a0 = [project(u, u, g=0) for u in range(3)]
+        a1 = [project(u, 3 + u, g=1) for u in range(3)]
+        a2 = [project(u, 6 + u, g=2) for u in range(2)]
+        for u in range(3):
+            copy_out(a0[u], a0_copy[u])
+        for u in range(2):
+            combine(early[:, u], a1[u], a0_copy[u], ALU.max)
+        prepare_c(1, tag="wc1")
+        late = keep.tile([P, 6, CHUNK, PACK], F32, name="late", tag="c1", align_bytes=64)
+        after_c = keep.tile([P, 2, CHUNK, PACK], F32, name="after_c", tag="c_bf1", align_bytes=64)
+        partial = [early[:, 0], early[:, 1], after_c[:, 0], after_c[:, 1]]
+        pooled = [late[:, u] for u in range(3)]
+        own_copy = [late[:, 3], late[:, 4]]
+        last_copy = late[:, 5]
+        own = [project(u, u, own=True) for u in range(2)]
+        a2.append(project(2, 3, g=2))
+        total = [keep.tile([P, CHUNK, PACK], F32, name="total%d" % u, align_bytes=64) for u in range(3)]
+        for u in range(2):
+            copy_out(own[u], own_copy[u])
+        combine(pooled[0], a2[0], partial[0], ALU.max)
+        combine(partial[2], a1[2], a0_copy[2], ALU.max)
+        combine(pooled[1], a2[1], partial[1], ALU.max)
+        combine(pooled[2], a2[2], partial[2], ALU.max)
+        for u in range(2):
+            nc.gpsimd.tensor_tensor(out=total[u][:], in0=pooled[u], in1=own_copy[u], op=ALU.add)
+        copy_out(project(3, 2, g=0, own=True), last_copy)
+        combine(partial[3], project(3, 4, g=1, own=True), last_copy, ALU.max)
+        combine(total[2][:], project(2, 0, own=True), pooled[2], ALU.add)
+        for u in range(3):
+            nc.scalar.activation(out=h_chunk(u), in_=total[u][:], func=ACT.Relu)
         nc.vector.scalar_tensor_tensor(
-            out=h_chunk(3), in0=by_point(last), scalar=0.0, in1=partial3[:], op0=ALU.max, op1=ALU.max
+            out=h_chunk(3),
+            in0=by_point(project(3, 7, g=2, own=True)),
+            scalar=0.0,
+            in1=partial[3],
+            op0=ALU.max,
+            op1=ALU.max,
         )
-
-        finish(0, y0, 0, step=1)
-        y1 = second_layer(1)
+        y0 = second_layer(0, (6, 1))
+        y1 = second_layer(1, (5, 3))
+        finish(0, y0, 0, step=BLOCKS_PER_BANK)
         finish(0, y0, 1, step=BLOCKS_PER_BANK)
         finish(1, y1, 0, step=BLOCKS_PER_BANK)
         finish(1, y1, 1, step=1)

@@ -23,12 +23,11 @@ PER_COLUMN = 16
 LINE = 4
 CHUNK = 128
 HALF = 256
-BLOCKS_PER_BANK = 2
 
 
-def load_plane(nc, plane, rows):
+def load_plane(queues, plane, rows):
     for quadrant in range(4):
-        nc.sync.dma_start(
+        queues[quadrant % len(queues)].dma_start(
             out=plane[32 * quadrant : 32 * quadrant + 4, :].bitcast(I32),
             in_=rows[4 * quadrant : 4 * quadrant + 4, :].bitcast(I32),
         )
@@ -59,14 +58,14 @@ def tile_list_pnet_res_kernel(
         w_raw = keep.tile([P, 2 * R], U8, name="w_raw", align_bytes=64)
         nc.sync.dma_start(out=w_raw[:].bitcast(I32), in_=w_words[0].bitcast(I32))
         table = keep.tile([P, T], I32, name="table", align_bytes=64)
-        load_plane(nc, tab_plane, tab_scales[0])
+        load_plane((nc.sync, nc.scalar), tab_plane, tab_scales[0])
         nc.sync.dma_start(out=table[:], in_=tab_words[0].rearrange("p t i -> p (t i)").bitcast(I32))
-        load_plane(nc, w_plane_raw, w_scales[0])
+        load_plane((nc.sync,), w_plane_raw, w_scales[0])
         wc_raw = [load_half("wc", wc, half) for half in range(2)]
         c_raw = [load_half("c", c, half) for half in range(2)]
         wd_codes = keep.tile([P, N], I32, name="wd_codes", align_bytes=64)
         nc.sync.dma_start(out=wd_codes[:], in_=wd_words[0].rearrange("p n i -> p (n i)").bitcast(I32))
-        load_plane(nc, wd_plane, wd_scales[0])
+        load_plane((nc.sync,), wd_plane, wd_scales[0])
         res_rows = res.rearrange("(b p) j -> p b j", p=P)
         out_rows = out.rearrange("(b p) j -> p b j", p=P)
         res_sb = []
@@ -125,11 +124,6 @@ def tile_list_pnet_res_kernel(
         def project(u, bank_number, g=None, own=False):
             bank = psum.tile([P, PACK, CHUNK], F32, name="bank", tag="bank%d" % bank_number)
             passes = []
-            if g is not None:
-                moving = picked[g, u].bitcast(FP8X4)
-                scales = picked_plane[:, g * J + u * CHUNK : g * J + (u + 1) * CHUNK]
-                for t in range(PACK):
-                    passes.append((t, w_codes[:, t, :].bitcast(FP4X4), w_plane[:, t, :], moving, scales))
             if own:
                 half, start = divmod(u * CHUNK, HALF)
                 c_codes, c_plane = c_mx[half]
@@ -138,6 +132,11 @@ def tile_list_pnet_res_kernel(
                 for t in range(PACK):
                     run = slice(t * P, (t + 1) * P)
                     passes.append((t, wc_codes[:, run].bitcast(FP8X4), wc_plane[:, run], moving, scales))
+            if g is not None:
+                moving = picked[g, u].bitcast(FP8X4)
+                scales = picked_plane[:, g * J + u * CHUNK : g * J + (u + 1) * CHUNK]
+                for t in range(PACK):
+                    passes.append((t, w_codes[:, t, :].bitcast(FP4X4), w_plane[:, t, :], moving, scales))
             lone = len(passes) == PACK
             for number, (t, lhs, lhs_scales, rhs, rhs_scales) in enumerate(passes):
                 nc.tensor.matmul_mx(
@@ -157,12 +156,12 @@ def tile_list_pnet_res_kernel(
         def combine(result, bank, other, op):
             nc.vector.tensor_tensor(out=result, in0=by_point(bank), in1=other, op=op)
 
-        def second_layer(half, bank_numbers):
-            h_codes, h_plane = quantize("h%d" % half, h_bf[half][:].rearrange("p j t -> p (j t)"), HALF)
+        def second_layer(half, plan, tag=None):
+            h_codes, h_plane = quantize("h%d" % half, h_bf[half], HALF, tag)
             banks = []
-            for number, first_block in zip(bank_numbers, range(0, N // P, BLOCKS_PER_BANK)):
-                y = psum.tile([P, BLOCKS_PER_BANK, HALF], F32, name="y", tag="bank%d" % number)
-                for b in range(BLOCKS_PER_BANK):
+            for number, first_block, blocks in plan:
+                y = psum.tile([P, blocks, HALF], F32, name="y", tag="bank%d" % number)
+                for b in range(blocks):
                     rows = slice((first_block + b) * P, (first_block + b + 1) * P)
                     nc.tensor.matmul_mx(
                         out=y[:, b, :],
@@ -176,74 +175,76 @@ def tile_list_pnet_res_kernel(
                 banks.append(y)
             return banks
 
-        def finish(half, banks, bank_number, step, on_gpsimd=False):
-            for b in range(0, BLOCKS_PER_BANK, step):
-                block = bank_number * BLOCKS_PER_BANK + b
-                result = keep.tile([P, step, HALF], F32, name="result%d_%d" % (half, block))
-                y = banks[bank_number][:, b : b + step, :]
-                residual = res_sb[half][:, block : block + step, :]
-                if on_gpsimd:
-                    copy = keep.tile([P, step, HALF], F32, name="y_copy%d_%d" % (half, block))
-                    nc.scalar.activation(out=copy[:], in_=y, func=ACT.Copy)
-                    nc.gpsimd.tensor_tensor(out=result[:], in0=copy[:], in1=residual, op=ALU.add)
-                else:
-                    nc.vector.tensor_tensor(out=result[:], in0=y, in1=residual, op=ALU.add)
-                nc.sync.dma_start(
-                    out=out_rows[:, block : block + step, half * HALF : (half + 1) * HALF], in_=result[:]
-                )
+        def finish(half, y, block, blocks, on_gpsimd=False):
+            result = keep.tile([P, blocks, HALF], F32, name="result%d_%d" % (half, block))
+            residual = res_sb[half][:, block : block + blocks, :]
+            if on_gpsimd:
+                copy = keep.tile([P, blocks, HALF], F32, name="y_copy%d_%d" % (half, block))
+                nc.scalar.activation(out=copy[:], in_=y, func=ACT.Copy)
+                nc.gpsimd.tensor_tensor(out=result[:], in0=copy[:], in1=residual, op=ALU.add)
+            else:
+                nc.vector.tensor_tensor(out=result[:], in0=y, in1=residual, op=ALU.add)
+            queue = nc.scalar if on_gpsimd else nc.sync
+            queue.dma_start(out=out_rows[:, block : block + blocks, half * HALF : (half + 1) * HALF], in_=result[:])
 
-        h_bf = [keep.tile([P, HALF, PACK], BF16, name="h_bf%d" % half, align_bytes=64) for half in range(2)]
 
         def h_chunk(u):
             half, start = divmod(u * CHUNK, HALF)
-            return h_bf[half][:, start : start + CHUNK, :]
+            return h_bf[half][:, start * PACK : (start + CHUNK) * PACK].rearrange("p (j t) -> p j t", t=PACK)
 
-        prepare_c(0)
-        first_copy = keep.tile([P, CHUNK, PACK], F32, name="first_copy", tag="wc1", align_bytes=64)
-        next_copies = keep.tile([P, 2, CHUNK, PACK], F32, name="next_copies", tag="wc0", align_bytes=64)
-        a0_copy = [first_copy[:], next_copies[:, 0], next_copies[:, 1]]
-        early = keep.tile([P, 2, CHUNK, PACK], F32, name="early", tag="c0", align_bytes=64)
+        def chunk_tile(name, count, tag=None):
+            tile = keep.tile([P, count, CHUNK, PACK], F32, name=name, tag=tag or name, align_bytes=64)
+            return [tile[:, n] for n in range(count)]
+
         a0 = [project(u, u, g=0) for u in range(3)]
         a1 = [project(u, 3 + u, g=1) for u in range(3)]
         a2 = [project(u, 6 + u, g=2) for u in range(2)]
-        for u in range(3):
-            copy_out(a0[u], a0_copy[u])
-        for u in range(2):
-            combine(early[:, u], a1[u], a0_copy[u], ALU.max)
-        prepare_c(1, tag="wc1")
-        late = keep.tile([P, 6, CHUNK, PACK], F32, name="late", tag="c1", align_bytes=64)
-        after_c = keep.tile([P, 2, CHUNK, PACK], F32, name="after_c", tag="c_bf1", align_bytes=64)
-        partial = [early[:, 0], early[:, 1], after_c[:, 0], after_c[:, 1]]
-        pooled = [late[:, u] for u in range(3)]
-        own_copy = [late[:, 3], late[:, 4]]
-        last_copy = late[:, 5]
-        own = [project(u, u, own=True) for u in range(2)]
+        (copy0,) = chunk_tile("copy0", 1, "wc1")
+        (copy1,) = chunk_tile("copy1", 1, "wc0")
+        partial0, partial3 = chunk_tile("partial", 2)
+        copy_out(a0[0], copy0)
+        copy_out(a0[1], copy1)
+        combine(partial0, a1[0], copy0, ALU.max)
+        prepare_c(0)
+        partial1, pooled0, partial2 = chunk_tile("after_c0", 3, "c0")
+        combine(partial1, a1[1], copy1, ALU.max)
+        combine(pooled0, a2[0], partial0, ALU.max)
+        prepare_c(1, tag="wc0")
+        copy2, own_copy0, own_copy1, pooled1, pooled2 = chunk_tile("after_c1", 5, "c1")
+        (copy3,) = chunk_tile("copy3", 1)
+        copy_out(a0[2], copy2)
+        copy_out(project(0, 0, own=True), own_copy0)
+        own1 = project(1, 1, own=True)
+        first, second = slice(0, CHUNK // 2), slice(CHUNK // 2, CHUNK)
+        nc.scalar.activation(out=own_copy1[:, first], in_=by_point(own1)[:, first], func=ACT.Copy)
         a2.append(project(2, 3, g=2))
-        total = [keep.tile([P, CHUNK, PACK], F32, name="total%d" % u, align_bytes=64) for u in range(3)]
-        for u in range(2):
-            copy_out(own[u], own_copy[u])
-        combine(pooled[0], a2[0], partial[0], ALU.max)
-        combine(partial[2], a1[2], a0_copy[2], ALU.max)
-        combine(pooled[1], a2[1], partial[1], ALU.max)
-        combine(pooled[2], a2[2], partial[2], ALU.max)
-        for u in range(2):
-            nc.gpsimd.tensor_tensor(out=total[u][:], in0=pooled[u], in1=own_copy[u], op=ALU.add)
-        copy_out(project(3, 2, g=0, own=True), last_copy)
-        combine(partial[3], project(3, 4, g=1, own=True), last_copy, ALU.max)
-        combine(total[2][:], project(2, 0, own=True), pooled[2], ALU.add)
-        for u in range(3):
-            nc.scalar.activation(out=h_chunk(u), in_=total[u][:], func=ACT.Relu)
+        combine(partial2, a1[2], copy2, ALU.max)
+        combine(pooled1, a2[1], partial1, ALU.max)
+        combine(pooled2, a2[2], partial2, ALU.max)
+        (total0,) = chunk_tile("total0", 1, "c_bf1")
+        row = keep.tile([P, 3 * CHUNK * PACK], BF16, name="row", align_bytes=64)
+        total1 = row[:, CHUNK * PACK :].bitcast(F32).rearrange("p (j t) -> p j t", t=PACK)
+        nc.gpsimd.tensor_tensor(out=total0, in0=pooled0, in1=own_copy0, op=ALU.add)
+        nc.gpsimd.tensor_tensor(out=total1[:, first], in0=pooled1[:, first], in1=own_copy1[:, first], op=ALU.add)
+        nc.vector.tensor_tensor(out=total1[:, second], in0=by_point(own1)[:, second], in1=pooled1[:, second], op=ALU.add)
+        copy_out(project(3, 2, g=0, own=True), copy3)
+        combine(partial3, project(3, 4, g=1, own=True), copy3, ALU.max)
+        h_first = keep.tile([P, HALF * PACK], BF16, name="h_first", tag="g0", align_bytes=64)
+        h_bf = [h_first[:], row[:, : HALF * PACK]]
+        combine(h_chunk(2), project(2, 2, own=True), pooled2, ALU.add)
+        nc.scalar.activation(out=h_chunk(0), in_=total0, func=ACT.Relu)
+        nc.scalar.activation(out=h_chunk(1), in_=total1, func=ACT.Relu)
+        last = project(3, 3, g=2, own=True)
+        y0 = second_layer(0, ((1, 2, 2), (6, 0, 1), (0, 1, 1)), "c1")
         nc.vector.scalar_tensor_tensor(
-            out=h_chunk(3),
-            in0=by_point(project(3, 7, g=2, own=True)),
-            scalar=0.0,
-            in1=partial[3],
-            op0=ALU.max,
-            op1=ALU.max,
+            out=h_chunk(3), in0=by_point(last), scalar=0.0, in1=partial3, op0=ALU.max, op1=ALU.max
         )
-        y0 = second_layer(0, (6, 1))
-        y1 = second_layer(1, (5, 3))
-        finish(0, y0, 0, step=BLOCKS_PER_BANK)
-        finish(0, y0, 1, step=BLOCKS_PER_BANK)
-        finish(1, y1, 0, step=BLOCKS_PER_BANK)
-        finish(1, y1, 1, step=1)
+        nc.vector.tensor_scalar(out=h_chunk(2), in0=h_chunk(2), scalar1=0.0, scalar2=None, op0=ALU.max)
+        finish(0, y0[0][:, 0:1], 2, 1)
+        y1 = second_layer(1, ((5, 0, 2), (7, 2, 2)))
+        finish(0, y0[1][:], 0, 1, on_gpsimd=True)
+        finish(0, y0[0][:, 1:2], 3, 1)
+        finish(0, y0[2][:], 1, 1)
+        finish(1, y1[0][:], 0, 2)
+        finish(1, y1[1][:, 0:1], 2, 1)
+        finish(1, y1[1][:, 1:2], 3, 1)

@@ -25,9 +25,9 @@ CHUNK = 128
 HALF = 256
 
 
-def load_plane(queues, plane, rows):
+def load_plane(nc, plane, rows):
     for quadrant in range(4):
-        queues[quadrant % len(queues)].dma_start(
+        nc.sync.dma_start(
             out=plane[32 * quadrant : 32 * quadrant + 4, :].bitcast(I32),
             in_=rows[4 * quadrant : 4 * quadrant + 4, :].bitcast(I32),
         )
@@ -58,14 +58,14 @@ def tile_list_pnet_res_kernel(
         w_raw = keep.tile([P, 2 * R], U8, name="w_raw", align_bytes=64)
         nc.sync.dma_start(out=w_raw[:].bitcast(I32), in_=w_words[0].bitcast(I32))
         table = keep.tile([P, T], I32, name="table", align_bytes=64)
-        load_plane((nc.sync, nc.scalar), tab_plane, tab_scales[0])
+        load_plane(nc, tab_plane, tab_scales[0])
         nc.sync.dma_start(out=table[:], in_=tab_words[0].rearrange("p t i -> p (t i)").bitcast(I32))
-        load_plane((nc.sync,), w_plane_raw, w_scales[0])
+        load_plane(nc, w_plane_raw, w_scales[0])
         wc_raw = [load_half("wc", wc, half) for half in range(2)]
         c_raw = [load_half("c", c, half) for half in range(2)]
         wd_codes = keep.tile([P, N], I32, name="wd_codes", align_bytes=64)
         nc.sync.dma_start(out=wd_codes[:], in_=wd_words[0].rearrange("p n i -> p (n i)").bitcast(I32))
-        load_plane((nc.sync,), wd_plane, wd_scales[0])
+        load_plane(nc, wd_plane, wd_scales[0])
         res_rows = res.rearrange("(b p) j -> p b j", p=P)
         out_rows = out.rearrange("(b p) j -> p b j", p=P)
         res_sb = []
@@ -222,24 +222,23 @@ def tile_list_pnet_res_kernel(
         combine(pooled1, a2[1], partial1, ALU.max)
         combine(pooled2, a2[2], partial2, ALU.max)
         (total0,) = chunk_tile("total0", 1, "c_bf1")
-        row = keep.tile([P, 3 * CHUNK * PACK], BF16, name="row", align_bytes=64)
-        total1 = row[:, CHUNK * PACK :].bitcast(F32).rearrange("p (j t) -> p j t", t=PACK)
+        (total1,) = chunk_tile("total1", 1)
         nc.gpsimd.tensor_tensor(out=total0, in0=pooled0, in1=own_copy0, op=ALU.add)
         nc.gpsimd.tensor_tensor(out=total1[:, first], in0=pooled1[:, first], in1=own_copy1[:, first], op=ALU.add)
         nc.vector.tensor_tensor(out=total1[:, second], in0=by_point(own1)[:, second], in1=pooled1[:, second], op=ALU.add)
         copy_out(project(3, 2, g=0, own=True), copy3)
         combine(partial3, project(3, 4, g=1, own=True), copy3, ALU.max)
-        h_first = keep.tile([P, HALF * PACK], BF16, name="h_first", tag="g0", align_bytes=64)
-        h_bf = [h_first[:], row[:, : HALF * PACK]]
+        row = keep.tile([P, 3 * CHUNK * PACK], BF16, name="row", tag="g0", align_bytes=64)
+        h_bf = [row[:, CHUNK * PACK :], row[:, : HALF * PACK]]
         combine(h_chunk(2), project(2, 2, own=True), pooled2, ALU.add)
         nc.scalar.activation(out=h_chunk(0), in_=total0, func=ACT.Relu)
         nc.scalar.activation(out=h_chunk(1), in_=total1, func=ACT.Relu)
         last = project(3, 3, g=2, own=True)
         y0 = second_layer(0, ((1, 2, 2), (6, 0, 1), (0, 1, 1)), "c1")
+        nc.vector.tensor_scalar(out=h_chunk(2), in0=h_chunk(2), scalar1=0.0, scalar2=None, op0=ALU.max)
         nc.vector.scalar_tensor_tensor(
             out=h_chunk(3), in0=by_point(last), scalar=0.0, in1=partial3, op0=ALU.max, op1=ALU.max
         )
-        nc.vector.tensor_scalar(out=h_chunk(2), in0=h_chunk(2), scalar1=0.0, scalar2=None, op0=ALU.max)
         finish(0, y0[0][:, 0:1], 2, 1)
         y1 = second_layer(1, ((5, 0, 2), (7, 2, 2)))
         finish(0, y0[1][:], 0, 1, on_gpsimd=True)

@@ -26,11 +26,8 @@ HALF = 256
 
 
 def load_plane(nc, plane, rows):
-    for quadrant in range(4):
-        nc.sync.dma_start(
-            out=plane[32 * quadrant : 32 * quadrant + 4, :].bitcast(I32),
-            in_=rows[4 * quadrant : 4 * quadrant + 4, :].bitcast(I32),
-        )
+    for r in range(4):
+        nc.sync.dma_start(out=plane[r:P:32, :].bitcast(I32), in_=rows[r:16:4, :].bitcast(I32))
 
 
 def tile_list_pnet_res_kernel(

@@ -118,7 +118,7 @@ def tile_list_pnet_res_kernel(
         def by_point(bank):
             return bank[:].rearrange("p t j -> p j t")
 
-        def project(u, bank_number, g=None, own=False):
+        def project(u, bank_number, g=None, own=False, own_last=False):
             bank = psum.tile([P, PACK, CHUNK], F32, name="bank", tag="bank%d" % bank_number)
             passes = []
             if own:
@@ -134,6 +134,8 @@ def tile_list_pnet_res_kernel(
                 scales = picked_plane[:, g * J + u * CHUNK : g * J + (u + 1) * CHUNK]
                 for t in range(PACK):
                     passes.append((t, w_codes[:, t, :].bitcast(FP4X4), w_plane[:, t, :], moving, scales))
+            if own_last:
+                passes = passes[PACK:] + passes[:PACK]
             lone = len(passes) == PACK
             for number, (t, lhs, lhs_scales, rhs, rhs_scales) in enumerate(passes):
                 nc.tensor.matmul_mx(
@@ -172,9 +174,10 @@ def tile_list_pnet_res_kernel(
                 banks.append(y)
             return banks
 
-        def finish(half, y, block, blocks, on_gpsimd=False):
-            result = keep.tile([P, blocks, HALF], F32, name="result%d_%d" % (half, block))
-            residual = res_sb[half][:, block : block + blocks, :]
+        def finish(half, y, block, blocks, on_gpsimd=False, start=0, width=HALF):
+            result = keep.tile([P, blocks, width], F32, name="result%d_%d_%d" % (half, block, start))
+            residual = res_sb[half][:, block : block + blocks, start : start + width]
+            y = y[:, :, start : start + width]
             if on_gpsimd:
                 copy = keep.tile([P, blocks, HALF], F32, name="y_copy%d_%d" % (half, block))
                 nc.scalar.activation(out=copy[:], in_=y, func=ACT.Copy)
@@ -182,7 +185,7 @@ def tile_list_pnet_res_kernel(
             else:
                 nc.vector.tensor_tensor(out=result[:], in0=y, in1=residual, op=ALU.add)
             queue = nc.scalar if on_gpsimd else nc.sync
-            queue.dma_start(out=out_rows[:, block : block + blocks, half * HALF : (half + 1) * HALF], in_=result[:])
+            queue.dma_start(out=out_rows[:, block : block + blocks, half * HALF + start : half * HALF + start + width], in_=result[:])
 
 
         def h_chunk(u):
@@ -198,7 +201,8 @@ def tile_list_pnet_res_kernel(
         a2 = [project(u, 6 + u, g=2) for u in range(2)]
         (copy0,) = chunk_tile("copy0", 1, "wc1")
         (copy1,) = chunk_tile("copy1", 1, "wc0")
-        partial0, partial3 = chunk_tile("partial", 2)
+        (partial0,) = chunk_tile("partial0", 1)
+        rounded = keep.tile([P, 2, CHUNK, PACK], BF16, name="rounded", align_bytes=64)
         copy_out(a0[0], copy0)
         copy_out(a0[1], copy1)
         combine(partial0, a1[0], copy0, ALU.max)
@@ -223,24 +227,31 @@ def tile_list_pnet_res_kernel(
         nc.gpsimd.tensor_tensor(out=total0, in0=pooled0, in1=own_copy0, op=ALU.add)
         nc.gpsimd.tensor_tensor(out=total1[:, first], in0=pooled1[:, first], in1=own_copy1[:, first], op=ALU.add)
         nc.vector.tensor_tensor(out=total1[:, second], in0=by_point(own1)[:, second], in1=pooled1[:, second], op=ALU.add)
-        copy_out(project(3, 2, g=0, own=True), copy3)
-        combine(partial3, project(3, 4, g=1, own=True), copy3, ALU.max)
-        row = keep.tile([P, 3 * CHUNK * PACK], BF16, name="row", tag="g0", align_bytes=64)
-        h_bf = [row[:, CHUNK * PACK :], row[:, : HALF * PACK]]
-        combine(h_chunk(2), project(2, 2, own=True), pooled2, ALU.add)
+        copy_out(project(3, 4, g=0, own=True, own_last=True), copy3)
+        copy_out(project(3, 6, g=2, own=True, own_last=True), rounded[:, 1])
+        nc.vector.scalar_tensor_tensor(
+            out=rounded[:, 0],
+            in0=by_point(project(3, 2, g=1, own=True)),
+            scalar=0.0,
+            in1=copy3,
+            op0=ALU.max,
+            op1=ALU.max,
+        )
+        h_first = keep.tile([P, HALF * PACK], BF16, name="h_first", tag="g1", align_bytes=64)
+        h_second = keep.tile([P, HALF * PACK], BF16, name="h_second", align_bytes=64)
+        h_bf = [h_first[:], h_second[:]]
+        combine(h_chunk(2), project(2, 4, own=True), pooled2, ALU.add)
         nc.scalar.activation(out=h_chunk(0), in_=total0, func=ACT.Relu)
         nc.scalar.activation(out=h_chunk(1), in_=total1, func=ACT.Relu)
-        last = project(3, 3, g=2, own=True)
-        y0 = second_layer(0, ((1, 2, 2), (6, 0, 1), (0, 1, 1)), "c1")
+        nc.vector.tensor_tensor(out=h_chunk(3), in0=rounded[:, 0], in1=rounded[:, 1], op=ALU.max)
         nc.vector.tensor_scalar(out=h_chunk(2), in0=h_chunk(2), scalar1=0.0, scalar2=None, op0=ALU.max)
-        nc.vector.scalar_tensor_tensor(
-            out=h_chunk(3), in0=by_point(last), scalar=0.0, in1=partial3, op0=ALU.max, op1=ALU.max
-        )
-        finish(0, y0[0][:, 0:1], 2, 1)
-        y1 = second_layer(1, ((5, 0, 2), (7, 2, 2)))
+        y0 = second_layer(0, ((1, 2, 1), (6, 0, 1), (3, 3, 1), (0, 1, 1)), "c1")
+        y1 = second_layer(1, ((5, 0, 1), (2, 1, 1), (7, 2, 2)), "total1")
+        finish(0, y0[0][:], 2, 1)
         finish(0, y0[1][:], 0, 1, on_gpsimd=True)
-        finish(0, y0[0][:, 1:2], 3, 1)
-        finish(0, y0[2][:], 1, 1)
-        finish(1, y1[0][:], 0, 2)
-        finish(1, y1[1][:, 0:1], 2, 1)
-        finish(1, y1[1][:, 1:2], 3, 1)
+        finish(0, y0[2][:], 3, 1)
+        finish(0, y0[3][:], 1, 1)
+        finish(1, y1[0][:], 0, 1)
+        finish(1, y1[1][:], 1, 1)
+        finish(1, y1[2][:, 0:1], 2, 1)
+        finish(1, y1[2][:, 1:2], 3, 1)

@@ -57,8 +57,9 @@ def tile_list_pnet_res_kernel(
         table = keep.tile([P, T], I32, name="table", align_bytes=64)
         load_plane(nc, tab_plane, tab_scales[0])
         nc.sync.dma_start(out=table[:], in_=tab_words[0].rearrange("p t i -> p (t i)").bitcast(I32))
+        wc_raw = [load_half("wc", wc, 0)]
         load_plane(nc, w_plane_raw, w_scales[0])
-        wc_raw = [load_half("wc", wc, half) for half in range(2)]
+        wc_raw.append(load_half("wc", wc, 1))
         c_raw = [load_half("c", c, half) for half in range(2)]
         wd_codes = keep.tile([P, N], I32, name="wd_codes", align_bytes=64)
         nc.sync.dma_start(out=wd_codes[:], in_=wd_words[0].rearrange("p n i -> p (n i)").bitcast(I32))

@@ -85,7 +85,7 @@ def tile_list_pnet_res_kernel(
             entries = offsets[:, (g * J + first) // PER_COLUMN : (g * J + first + count) // PER_COLUMN]
             nc.vector.tensor_copy(words[:], table[:].bitcast(U32).indirect(entries))
             for start in range(0, count, CHUNK):
-                picked[g, (first + start) // CHUNK] = words[:, start : start + CHUNK]
+                picked[divmod((g * J + first + start) // CHUNK, J // CHUNK)] = words[:, start : start + CHUNK]
 
         def quantize(name, values, width, tag=None):
             codes = keep.tile([P, width], U32, name=name + "_codes", tag=tag or name + "_codes", align_bytes=64)
@@ -185,7 +185,7 @@ def tile_list_pnet_res_kernel(
                 nc.gpsimd.tensor_tensor(out=result[:], in0=copy[:], in1=residual, op=ALU.add)
             else:
                 nc.vector.tensor_tensor(out=result[:], in0=y, in1=residual, op=ALU.add)
-            queue = nc.scalar if on_gpsimd else nc.sync
+            queue = nc.scalar if on_gpsimd or block == 3 or (half, block) == (1, 1) else nc.sync
             queue.dma_start(out=out_rows[:, block : block + blocks, half * HALF + start : half * HALF + start + width], in_=result[:])
 
 
@@ -247,12 +247,12 @@ def tile_list_pnet_res_kernel(
         nc.vector.tensor_tensor(out=h_chunk(3), in0=rounded[:, 0], in1=rounded[:, 1], op=ALU.max)
         nc.vector.tensor_scalar(out=h_chunk(2), in0=h_chunk(2), scalar1=0.0, scalar2=None, op0=ALU.max)
         y0 = second_layer(0, ((1, 2, 1), (6, 0, 1), (3, 3, 1), (0, 1, 1)), "c1")
-        y1 = second_layer(1, ((5, 0, 1), (2, 1, 1), (7, 2, 2)), "total1")
+        y1 = second_layer(1, ((5, 0, 1), (2, 1, 1), (7, 2, 1), (4, 3, 1)), "total1")
         finish(0, y0[0][:], 2, 1)
         finish(0, y0[1][:], 0, 1, on_gpsimd=True)
         finish(0, y0[2][:], 3, 1)
         finish(0, y0[3][:], 1, 1)
         finish(1, y1[0][:], 0, 1)
         finish(1, y1[1][:], 1, 1)
-        finish(1, y1[2][:, 0:1], 2, 1)
-        finish(1, y1[2][:, 1:2], 3, 1)
+        finish(1, y1[2][:], 2, 1)
+        finish(1, y1[3][:], 3, 1)

@@ -57,10 +57,11 @@ def tile_list_pnet_res_kernel(
         table = keep.tile([P, T], I32, name="table", align_bytes=64)
         load_plane(nc, tab_plane, tab_scales[0])
         nc.sync.dma_start(out=table[:], in_=tab_words[0].rearrange("p t i -> p (t i)").bitcast(I32))
-        wc_raw = [load_half("wc", wc, 0)]
         load_plane(nc, w_plane_raw, w_scales[0])
+        wc_raw = [load_half("wc", wc, 0)]
+        c_raw = [load_half("c", c, 0)]
         wc_raw.append(load_half("wc", wc, 1))
-        c_raw = [load_half("c", c, half) for half in range(2)]
+        c_raw.append(load_half("c", c, 1))
         wd_codes = keep.tile([P, N], I32, name="wd_codes", align_bytes=64)
         nc.sync.dma_start(out=wd_codes[:], in_=wd_words[0].rearrange("p n i -> p (n i)").bitcast(I32))
         load_plane(nc, wd_plane, wd_scales[0])
@@ -77,8 +78,9 @@ def tile_list_pnet_res_kernel(
         w_plane = keep.tile([P, PACK, P], U8, name="w_plane", align_bytes=64)
         nc.gpsimd.tensor_copy(w_plane[:], w_plane_raw[:].rearrange("p (m t) -> p t m", t=PACK))
 
-        picked_plane = keep.tile([P, G * J], U8, name="picked_plane", align_bytes=64)
-        nc.vector.tensor_copy(picked_plane[:], tab_plane[:].indirect(offsets[:]))
+        early = G * J - HALF
+        picked_plane = keep.tile([P, early], U8, name="picked_plane", align_bytes=64)
+        nc.vector.tensor_copy(picked_plane[:], tab_plane[:].indirect(offsets[:, 0 : early // PER_COLUMN]))
         picked = {}
         for g, first, count, tag in ((0, 0, HALF, "c_bf1"), (0, HALF, HALF, "g0"), (1, 0, J, "g1"), (2, 0, J, "g2")):
             words = keep.tile([P, count], U32, name="picked", tag=tag, align_bytes=64)
@@ -86,6 +88,9 @@ def tile_list_pnet_res_kernel(
             nc.vector.tensor_copy(words[:], table[:].bitcast(U32).indirect(entries))
             for start in range(0, count, CHUNK):
                 picked[divmod((g * J + first + start) // CHUNK, J // CHUNK)] = words[:, start : start + CHUNK]
+
+        late_plane = keep.tile([P, HALF], U8, name="late_plane", tag="w_plane_raw", align_bytes=64)
+        nc.vector.tensor_copy(late_plane[:], tab_plane[:].indirect(offsets[:, early // PER_COLUMN : G * J // PER_COLUMN]))
 
         def quantize(name, values, width, tag=None):
             codes = keep.tile([P, width], U32, name=name + "_codes", tag=tag or name + "_codes", align_bytes=64)
@@ -132,7 +137,9 @@ def tile_list_pnet_res_kernel(
                     passes.append((t, wc_codes[:, run].bitcast(FP8X4), wc_plane[:, run], moving, scales))
             if g is not None:
                 moving = picked[g, u].bitcast(FP8X4)
-                scales = picked_plane[:, g * J + u * CHUNK : g * J + (u + 1) * CHUNK]
+                entry = g * J + u * CHUNK
+                plane, entry = (picked_plane, entry) if entry < early else (late_plane, entry - early)
+                scales = plane[:, entry : entry + CHUNK]
                 for t in range(PACK):
                     passes.append((t, w_codes[:, t, :].bitcast(FP4X4), w_plane[:, t, :], moving, scales))
             if own_last:
@@ -200,15 +207,13 @@ def tile_list_pnet_res_kernel(
         a0 = [project(u, u, g=0) for u in range(3)]
         a1 = [project(u, 3 + u, g=1) for u in range(3)]
         a2 = [project(u, 6 + u, g=2) for u in range(2)]
-        (copy0,) = chunk_tile("copy0", 1, "wc1")
-        (copy1,) = chunk_tile("copy1", 1, "wc0")
-        (partial0,) = chunk_tile("partial0", 1)
+        copy0, copy1 = chunk_tile("after_wc0", 2, "wc0")
         rounded = keep.tile([P, 2, CHUNK, PACK], BF16, name="rounded", align_bytes=64)
         copy_out(a0[0], copy0)
         copy_out(a0[1], copy1)
-        combine(partial0, a1[0], copy0, ALU.max)
         prepare_c(0)
-        partial1, pooled0, partial2 = chunk_tile("after_c0", 3, "c0")
+        partial0, partial1, pooled0, partial2 = chunk_tile("after_c0", 4, "c0")
+        combine(partial0, a1[0], copy0, ALU.max)
         combine(partial1, a1[1], copy1, ALU.max)
         combine(pooled0, a2[0], partial0, ALU.max)
         prepare_c(1, tag="wc0")

from contextlib import ExitStack

import concourse.mybir as mybir

K, R, N, T, J = 512, 512, 512, 2048, 512
G = 3
FLOPS = 2 * J * (K * R * (G + 1) + R * N)

F32 = mybir.dt.float32
BF16 = mybir.dt.bfloat16
I32 = mybir.dt.int32
U32 = mybir.dt.uint32
U16 = mybir.dt.uint16
U8 = mybir.dt.uint8
FP8X4 = mybir.dt.float8_e4m3fn_x4
FP4X4 = mybir.dt.float4_e2m1fn_x4
ACT = mybir.ActivationFunctionType
ALU = mybir.AluOpType

P = 128
PACK = 4
PER_COLUMN = 16
LINE = 4
CHUNK = 128
HALF = 256


def load_plane(nc, plane, rows):
    for r in range(4):
        nc.sync.dma_start(out=plane[r:P:32, :].bitcast(I32), in_=rows[r:16:4, :].bitcast(I32))


def tile_list_pnet_res_kernel(
    tc, tab_words, tab_scales, c, w_words, w_scales, wc, wd_words, wd_scales, res, offs, out
):
    nc = tc.nc
    with ExitStack() as ctx:
        keep = ctx.enter_context(tc.tile_pool(name="keep", bufs=1))
        psum = ctx.enter_context(tc.psum_pool(name="psum", bufs=1))

        offsets = keep.tile([P, G * J // PER_COLUMN], U16, name="offsets")
        tab_plane = keep.tile([P, T], U8, name="tab_plane", align_bytes=64)
        w_plane_raw = keep.tile([P, R], U8, name="w_plane_raw", align_bytes=64)
        wd_plane = keep.tile([P, N], U8, name="wd_plane", align_bytes=64)
        for plane in (tab_plane, w_plane_raw, wd_plane):
            nc.vector.memset(plane[:].bitcast(I32), 0)

        def load_half(name, rows, half):
            raw = keep.tile([P, PACK, HALF], F32, name="raw", tag="%s%d" % (name, half), align_bytes=64)
            view = rows.rearrange("(p i) x -> p i x", i=PACK)
            nc.sync.dma_start(out=raw[:], in_=view[:, :, half * HALF : (half + 1) * HALF])
            return raw

        nc.sync.dma_start(offsets[:], offs)
        w_raw = keep.tile([P, 2 * R], U8, name="w_raw", align_bytes=64)
        nc.sync.dma_start(out=w_raw[:].bitcast(I32), in_=w_words[0].bitcast(I32))
        table = keep.tile([P, T], I32, name="table", align_bytes=64)
        load_plane(nc, tab_plane, tab_scales[0])
        nc.sync.dma_start(out=table[:], in_=tab_words[0].rearrange("p t i -> p (t i)").bitcast(I32))
        load_plane(nc, w_plane_raw, w_scales[0])
        wc_raw = [load_half("wc", wc, 0)]
        c_raw = [load_half("c", c, 0)]
        wc_raw.append(load_half("wc", wc, 1))
        c_raw.append(load_half("c", c, 1))
        wd_codes = keep.tile([P, N], I32, name="wd_codes", align_bytes=64)
        nc.sync.dma_start(out=wd_codes[:], in_=wd_words[0].rearrange("p n i -> p (n i)").bitcast(I32))
        load_plane(nc, wd_plane, wd_scales[0])
        res_rows = res.rearrange("(b p) j -> p b j", p=P)
        out_rows = out.rearrange("(b p) j -> p b j", p=P)
        res_sb = []
        for half in range(2):
            rows = keep.tile([P, N // P, HALF], F32, name="res%d" % half)
            nc.sync.dma_start(out=rows[:], in_=res_rows[:, :, half * HALF : (half + 1) * HALF])
            res_sb.append(rows)

        w_codes = keep.tile([P, PACK, P], U16, name="w_codes", align_bytes=64)
        nc.vector.tensor_copy(w_codes[:], w_raw[:].bitcast(U16).rearrange("p (m t) -> p t m", t=PACK))
        w_plane = keep.tile([P, PACK, P], U8, name="w_plane", align_bytes=64)
        nc.gpsimd.tensor_copy(w_plane[:], w_plane_raw[:].rearrange("p (m t) -> p t m", t=PACK))

        early = G * J - HALF
        picked_plane = keep.tile([P, early], U8, name="picked_plane", align_bytes=64)
        nc.vector.tensor_copy(picked_plane[:], tab_plane[:].indirect(offsets[:, 0 : early // PER_COLUMN]))
        picked = {}
        for g, first, count, tag in ((0, 0, HALF, "c_bf1"), (0, HALF, HALF, "g0"), (1, 0, J, "g1"), (2, 0, J, "g2")):
            words = keep.tile([P, count], U32, name="picked", tag=tag, align_bytes=64)
            entries = offsets[:, (g * J + first) // PER_COLUMN : (g * J + first + count) // PER_COLUMN]
            nc.vector.tensor_copy(words[:], table[:].bitcast(U32).indirect(entries))
            for start in range(0, count, CHUNK):
                picked[divmod((g * J + first + start) // CHUNK, J // CHUNK)] = words[:, start : start + CHUNK]

        late_plane = keep.tile([P, HALF], U8, name="late_plane", tag="w_plane_raw", align_bytes=64)
        nc.vector.tensor_copy(late_plane[:], tab_plane[:].indirect(offsets[:, early // PER_COLUMN : G * J // PER_COLUMN]))

        def quantize(name, values, width, tag=None):
            codes = keep.tile([P, width], U32, name=name + "_codes", tag=tag or name + "_codes", align_bytes=64)
            scales = keep.tile([P, width], U8, name=name + "_plane", align_bytes=64)
            nc.vector.quantize_mx(out=codes[:].bitcast(FP8X4), scales=scales[:], in_=values)
            return codes, scales

        wc_bf = keep.tile([P, PACK, P, PACK], BF16, name="wc_bf", align_bytes=64)
        for half in range(2):
            dealt = wc_bf[:, :, half * HALF // PACK : (half + 1) * HALF // PACK, :]
            nc.scalar.activation(
                out=dealt.rearrange("p t m i -> p m i t"),
                in_=wc_raw[half][:].rearrange("p i (m t) -> p m i t", t=PACK),
                func=ACT.Copy,
            )
        wc_codes, wc_plane = quantize("wc", wc_bf[:].rearrange("p t m i -> p (t m i)"), R)

        c_mx = []

        def prepare_c(half, tag=None):
            c_bf = keep.tile([P, HALF, PACK], BF16, name="c_bf", tag="c_bf%d" % half, align_bytes=64)
            if half == 0:
                rows = c_raw[half][:].rearrange("p i j -> p j i")
                nc.gpsimd.tensor_scalar(out=c_bf[:], in0=rows, scalar1=1.0, scalar2=0.0, op0=ALU.mult, op1=ALU.add)
            else:
                woven = c_bf[:].rearrange("p (x e) i -> p x i e", e=LINE)
                rows = c_raw[half][:].rearrange("p i (x e) -> p x i e", e=LINE)
                nc.scalar.activation(out=woven, in_=rows, func=ACT.Copy)
            c_mx.append(quantize("c%d" % half, c_bf[:].rearrange("p j i -> p (j i)"), HALF, tag))

        def by_point(bank):
            return bank[:].rearrange("p t j -> p j t")

        def project(u, bank_number, g=None, own=False, own_last=False):
            bank = psum.tile([P, PACK, CHUNK], F32, name="bank", tag="bank%d" % bank_number)
            passes = []
            if own:
                half, start = divmod(u * CHUNK, HALF)
                c_codes, c_plane = c_mx[half]
                moving = c_codes[:, start : start + CHUNK].bitcast(FP8X4)
                scales = c_plane[:, start : start + CHUNK]
                for t in range(PACK):
                    run = slice(t * P, (t + 1) * P)
                    passes.append((t, wc_codes[:, run].bitcast(FP8X4), wc_plane[:, run], moving, scales))
            if g is not None:
                moving = picked[g, u].bitcast(FP8X4)
                entry = g * J + u * CHUNK
                plane, entry = (picked_plane, entry) if entry < early else (late_plane, entry - early)
                scales = plane[:, entry : entry + CHUNK]
                for t in range(PACK):
                    passes.append((t, w_codes[:, t, :].bitcast(FP4X4), w_plane[:, t, :], moving, scales))
            if own_last:
                passes = passes[PACK:] + passes[:PACK]
            lone = len(passes) == PACK
            for number, (t, lhs, lhs_scales, rhs, rhs_scales) in enumerate(passes):
                nc.tensor.matmul_mx(
                    out=bank[:, t, :],
                    lhsT=lhs,
                    lhsT_scale=lhs_scales,
                    rhs=rhs,
                    rhs_scale=rhs_scales,
                    start=lone or number == 0,
                    stop=lone or number == len(passes) - 1,
                )
            return bank

        def copy_out(bank, copy):
            nc.scalar.activation(out=copy, in_=by_point(bank), func=ACT.Copy)

        def combine(result, bank, other, op):
            nc.vector.tensor_tensor(out=result, in0=by_point(bank), in1=other, op=op)

        def second_layer(half, plan, tag=None):
            h_codes, h_plane = quantize("h%d" % half, h_bf[half], HALF, tag)
            banks = []
            for number, first_block, blocks in plan:
                y = psum.tile([P, blocks, HALF], F32, name="y", tag="bank%d" % number)
                for b in range(blocks):
                    rows = slice((first_block + b) * P, (first_block + b + 1) * P)
                    nc.tensor.matmul_mx(
                        out=y[:, b, :],
                        lhsT=wd_codes[:, rows].bitcast(FP8X4),
                        lhsT_scale=wd_plane[:, rows],
                        rhs=h_codes[:].bitcast(FP8X4),
                        rhs_scale=h_plane[:],
                        start=True,
                        stop=True,
                    )
                banks.append(y)
            return banks

        def finish(half, y, block, blocks, on_gpsimd=False, start=0, width=HALF):
            result = keep.tile([P, blocks, width], F32, name="result%d_%d_%d" % (half, block, start))
            residual = res_sb[half][:, block : block + blocks, start : start + width]
            y = y[:, :, start : start + width]
            if on_gpsimd:
                copy = keep.tile([P, blocks, HALF], F32, name="y_copy%d_%d" % (half, block))
                nc.scalar.activation(out=copy[:], in_=y, func=ACT.Copy)
                nc.gpsimd.tensor_tensor(out=result[:], in0=copy[:], in1=residual, op=ALU.add)
            else:
                nc.vector.tensor_tensor(out=result[:], in0=y, in1=residual, op=ALU.add)
            queue = nc.scalar if on_gpsimd or block == 3 or (half, block) == (1, 1) else nc.sync
            queue.dma_start(out=out_rows[:, block : block + blocks, half * HALF + start : half * HALF + start + width], in_=result[:])


        def h_chunk(u):
            half, start = divmod(u * CHUNK, HALF)
            return h_bf[half][:, start * PACK : (start + CHUNK) * PACK].rearrange("p (j t) -> p j t", t=PACK)

        def chunk_tile(name, count, tag=None):
            tile = keep.tile([P, count, CHUNK, PACK], F32, name=name, tag=tag or name, align_bytes=64)
            return [tile[:, n] for n in range(count)]

        a0 = [project(u, u, g=0) for u in range(3)]
        a1 = [project(u, 3 + u, g=1) for u in range(3)]
        a2 = [project(u, 6 + u, g=2) for u in range(2)]
        copy0, copy1 = chunk_tile("after_wc0", 2, "wc0")
        rounded = keep.tile([P, 2, CHUNK, PACK], BF16, name="rounded", align_bytes=64)
        copy_out(a0[0], copy0)
        copy_out(a0[1], copy1)
        prepare_c(0)
        partial0, partial1, pooled0, partial2 = chunk_tile("after_c0", 4, "c0")
        combine(partial0, a1[0], copy0, ALU.max)
        combine(partial1, a1[1], copy1, ALU.max)
        combine(pooled0, a2[0], partial0, ALU.max)
        prepare_c(1, tag="wc0")
        copy2, own_copy0, own_copy1, pooled1, pooled2 = chunk_tile("after_c1", 5, "c1")
        (copy3,) = chunk_tile("copy3", 1)
        copy_out(a0[2], copy2)
        copy_out(project(0, 0, own=True), own_copy0)
        own1 = project(1, 1, own=True)
        first, second = slice(0, CHUNK // 2), slice(CHUNK // 2, CHUNK)
        nc.scalar.activation(out=own_copy1[:, first], in_=by_point(own1)[:, first], func=ACT.Copy)
        a2.append(project(2, 3, g=2))
        combine(partial2, a1[2], copy2, ALU.max)
        combine(pooled1, a2[1], partial1, ALU.max)
        combine(pooled2, a2[2], partial2, ALU.max)
        (total0,) = chunk_tile("total0", 1, "c_bf1")
        (total1,) = chunk_tile("total1", 1)
        nc.gpsimd.tensor_tensor(out=total0, in0=pooled0, in1=own_copy0, op=ALU.add)
        nc.gpsimd.tensor_tensor(out=total1[:, first], in0=pooled1[:, first], in1=own_copy1[:, first], op=ALU.add)
        nc.vector.tensor_tensor(out=total1[:, second], in0=by_point(own1)[:, second], in1=pooled1[:, second], op=ALU.add)
        copy_out(project(3, 4, g=0, own=True, own_last=True), copy3)
        copy_out(project(3, 6, g=2, own=True, own_last=True), rounded[:, 1])
        nc.vector.scalar_tensor_tensor(
            out=rounded[:, 0],
            in0=by_point(project(3, 2, g=1, own=True)),
            scalar=0.0,
            in1=copy3,
            op0=ALU.max,
            op1=ALU.max,
        )
        h_first = keep.tile([P, HALF * PACK], BF16, name="h_first", tag="g1", align_bytes=64)
        h_second = keep.tile([P, HALF * PACK], BF16, name="h_second", align_bytes=64)
        h_bf = [h_first[:], h_second[:]]
        combine(h_chunk(2), project(2, 4, own=True), pooled2, ALU.add)
        nc.scalar.activation(out=h_chunk(0), in_=total0, func=ACT.Relu)
        nc.scalar.activation(out=h_chunk(1), in_=total1, func=ACT.Relu)
        nc.vector.tensor_tensor(out=h_chunk(3), in0=rounded[:, 0], in1=rounded[:, 1], op=ALU.max)
        nc.vector.tensor_scalar(out=h_chunk(2), in0=h_chunk(2), scalar1=0.0, scalar2=None, op0=ALU.max)
        y0 = second_layer(0, ((1, 2, 1), (6, 0, 1), (3, 3, 1), (0, 1, 1)), "c1")
        y1 = second_layer(1, ((5, 0, 1), (2, 1, 1), (7, 2, 1), (4, 3, 1)), "total1")
        finish(0, y0[0][:], 2, 1)
        finish(0, y0[1][:], 0, 1, on_gpsimd=True)
        finish(0, y0[2][:], 3, 1)
        finish(0, y0[3][:], 1, 1)
        finish(1, y1[0][:], 0, 1)
        finish(1, y1[1][:], 1, 1)
        finish(1, y1[2][:], 2, 1)
        finish(1, y1[3][:], 3, 1)
